import numpy as np, ml_dtypes
CORES = [9,25,41,57]
N = 4
BF = ml_dtypes.bfloat16
def gentries(a):
    return np.ascontiguousarray(a.reshape(8, 16, -1).transpose(0, 2, 1)).reshape(8, -1)
def gtable(e):
    e = np.asarray(e); return np.ascontiguousarray(e.reshape(8, -1, 16).transpose(0, 2, 1)).reshape(128, -1).astype(np.int32)
C, L, M, P, CAP, S, Q, RING = 128, 8192, 16, 256, 32, 2, 3, True
Z = 63 * S
def media(rng):
    return rng.integers(0, M, (N, 8, L)), rng.integers(-63, 64, (N, 8, 128 * M))
def zones(rng):
    t = rng.integers(CAP // 2, CAP + 1, (N, 8)); zr = rng.integers(0, t + 1)
    return np.roll(t - zr, 1, axis=0), zr, P - t - np.roll(t, 1, axis=0)
def crowd(rng, zl, zr, ni, near):
    n = zl + zr + ni; x = rng.integers(0, L, (N, 8, P))
    for r in range(N):
        for g in range(8):
            a = (near * rng.random(zl[r, g]) ** 2).astype(np.int64); b = L - 1 - (near * rng.random(zr[r, g]) ** 2).astype(np.int64)
            x[r, g, :n[r, g]] = rng.permutation(np.concatenate([a, b, rng.integers(Z, L - Z, ni[r, g])]))
    return x, n
def names(rng):
    return rng.integers(1, 2 ** 20, (N, 8, P)) * rng.choice(np.array([-1, 1]), (N, 8, P))
def pack(x, v, w, n, med, kick):
    d = {"x": np.stack([gtable(a) for a in x]), "v": np.stack([gtable(a) for a in v]), "w": np.stack([gtable(a) for a in w])}
    d["live"] = np.repeat(n, 16, axis=1)[:, :, None].astype(np.int32); d["med"] = med.astype(np.int32); d["kick"] = kick.astype(np.int32); return d
def plain(rng):
    zl, zr, room = zones(rng); x, n = crowd(rng, zl, zr, rng.integers(room // 3, room + 1), Z)
    return x, rng.integers(-63, 64, (N, 8, P)), names(rng), n
def setup_inputs(rng):
    return pack(*plain(rng), *media(rng))
def setup_inputs_full(rng):
    s = rng.permutation(np.array([1, 1, 1, 1, -1, -1, -1, -1])); right = np.where(s > 0, CAP, 0); left = CAP - right
    zr = np.tile(right, (N, 1)); zl = np.tile(left, (N, 1))
    if not RING:
        zr[N - 1] = 0; zl[0] = 0
    ni = P - zl - zr
    if not RING:
        ni[N - 1] -= right; ni[0] -= left
    x, n = crowd(rng, zl, zr, ni, 63); med, kick = media(rng); b = 63 * (S + 1)
    med[:, :, :b] = M - 1; med[:, :, L - b:] = M - 1
    for g in range(8):
        kick[:, g, 128 * (M - 1):] = 63 * s[g]
    return pack(x, rng.integers(-63, 64, (N, 8, P)), names(rng), n, med, kick)
def setup_inputs_both(rng):
    zl = np.full((N, 8), CAP); zr = np.full((N, 8), CAP)
    if not RING:
        zl[0] = 0; zr[N - 1] = 0
    x, n = crowd(rng, zl, zr, P - zl - zr, 63); med, kick = media(rng); b = 63 * (S + 1); e = 128 * (M - 1)
    med[:, :, :b] = M - 1; med[:, :, L - b:] = M - 1; kick[:, :, e:e + 64] = -63; kick[:, :, e + 64:] = 63
    side = np.where(x < 63, -1, np.where(x >= L - 63, 1, 0)); v = np.where(side == 0, rng.integers(-63, 64, x.shape), 63 * side); w = np.abs(names(rng))
    for r in range(N):
        for g in range(8):
            for s in (-1, 0, 1):
                k = np.flatnonzero(side[r, g] == s); w[r, g, k] = w[r, g, k] * rng.permutation(1 - 2 * (np.arange(k.size) & 1))
    return pack(x, v, w, n, med, kick)
def setup_inputs_empty(rng):
    x, v, w, n = plain(rng); o = rng.permutation(8); keep = rng.random((N, 8)) > 0.4; keep[:, o[2]] = True; n = np.where(keep, n, 0)
    n[:, o[:2]] = 0; n[rng.integers(0, N), o[0]] = 1
    return pack(x, v, w, n, *media(rng))
def setup_inputs_edges(rng):
    x, v, w, n = plain(rng); med, kick = media(rng); far = (x >= Z) & (x < L - Z)
    y = (x & -64) + 63 * rng.integers(0, 2, x.shape); x = np.where(far & (y >= Z) & (y < L - Z), y, x)
    x = np.where(far, x, np.where(x < Z, rng.choice(np.array([0, 0, 1, 62, 63, 64]), x.shape), L - 1 - rng.choice(np.array([0, 0, 1, 62, 63, 64]), x.shape)))
    v = rng.choice(np.array([-63, -1, 0, 1, 63]), v.shape); kick = np.where(rng.random(kick.shape) < 0.75, rng.choice(np.array([-63, -62, -1, 0, 1, 62, 63]), kick.shape), kick)
    s = rng.permutation(np.array([1, 1, 1, -1, -1, -1, 0, 0]))[None, :, None]; w = np.where(s == 0, w, np.abs(w) * s)
    return pack(x, v, w, n, med, kick)
def setup_inputs_spread(rng):
    zl, zr, room = zones(rng); x, n = crowd(rng, zl, zr, np.maximum(1, (room * rng.random((N, 8)) ** 4).astype(np.int64)), Z)
    w = np.minimum(np.exp2(20 * rng.random((N, 8, P))).astype(np.int64), 2 ** 20 - 1) * rng.choice(np.array([-1, 1]), (N, 8, P))
    v = np.rint(63 * (2 * rng.random((N, 8, P)) - 1) ** 5).astype(np.int64)
    med = np.repeat((M * rng.random((N, 8, L // 16)) ** 3).astype(np.int64), 16, axis=2); kick = np.rint(63 * (2 * rng.random((N, 8, 128 * M)) - 1) ** 3).astype(np.int64)
    return pack(x, v, w, n, med, kick)
def run(x, v, w, n, med, kick):
    worst, most = 0, int(n.max()); ri, gi = np.arange(N)[:, None, None], np.arange(8)[None, :, None]; sh = np.array([[L], [0], [0]])
    for s in range(S):
        on = np.arange(P) < n[:, :, None]; c = x >> 6
        ch = np.zeros((N, 8, C), np.int64); np.add.at(ch, (ri, gi, c), np.where(on, np.sign(w), 0))
        E = np.add.accumulate(ch.transpose(1, 0, 2).reshape(8, N * C), axis=1).reshape(8, N, C).transpose(1, 0, 2)
        u = np.clip(v + np.take_along_axis(E, c, axis=2), -63, 63)
        for i in range(Q):
            m = np.take_along_axis(med, (x + u) & (L - 1), axis=2); u = np.take_along_axis(kick, 128 * m + 64 + u, axis=2)
        x = x + u; v = u
        if not RING:
            k = x[0] < 0; x[0] = np.where(k, -1 - x[0], x[0]); v[0] = np.where(k, -v[0], v[0])
            k = x[N - 1] >= L; x[N - 1] = np.where(k, 2 * L - 1 - x[N - 1], x[N - 1]); v[N - 1] = np.where(k, -v[N - 1], v[N - 1])
        lf, rt = on & (x < 0), on & (x >= L); st = on & ~lf & ~rt
        worst = max(worst, int(np.sum(lf, axis=2).max()), int(np.sum(rt, axis=2).max()))
        t = np.stack([x, v, w]); new = np.zeros((3, N, 8, P), np.int64); cnt = np.zeros((N, 8), np.int64)
        for r in range(N):
            a, b = (r + N - 1) % N, (r + 1) % N
            for g in range(8):
                e = np.concatenate([t[:, r, g][:, st[r, g]], t[:, a, g][:, rt[a, g]] - sh, t[:, b, g][:, lf[b, g]] + sh], axis=1)
                most = max(most, e.shape[1]); cnt[r, g] = min(e.shape[1], P); new[:, r, g, :cnt[r, g]] = e[:, :P]
        x, v, w = new; n = cnt
    return x, v, w, worst, most
def state(x, v, w, live, med, kick):
    h = [np.stack([gentries(a) for a in z]).astype(np.int64) for z in (x, v, w)]
    return h + [live[:, ::16, 0].astype(np.int64), med.astype(np.int64), kick.astype(np.int64)]
def check_inputs(d):
    big = 2 ** 20 - 1
    bad = [k for k, lo, hi in (("x", 0, L - 1), ("v", -63, 63), ("w", -big, big), ("live", 0, P), ("med", 0, M - 1), ("kick", -63, 63)) if d[k].min() < lo or d[k].max() > hi]
    if (d["w"] == 0).any():
        bad.append("w")
    if (d["live"].reshape(N, 8, 16) != d["live"].reshape(N, 8, 16)[:, :, :1]).any():
        bad.append("live")
    if bad:
        return bad
    worst, most = run(*state(d["x"], d["v"], d["w"], d["live"], d["med"], d["kick"]))[3:]
    return (["leavers"] if worst > CAP else []) + (["places"] if most > P else [])
def reference(x, v, w, live, med, kick):
    xe, ve, we, worst, most = run(*state(x, v, w, live, med, kick))
    return {"yx": np.stack([gtable(a) for a in xe]).astype(np.float32), "yv": np.stack([gtable(a) for a in ve]).astype(np.float32), "yw": np.stack([gtable(a) for a in we]).astype(np.float32)}

@@ -1,0 +1,595 @@
+import numpy as np
+from concourse.bass import DstId, RemoteDMATransfer
+from concourse.mybir import AluOpType as A, ActivationFunctionType as F
+
+NS1, NS2 = 5, 12
+CUT1, CUT2 = (0, 8, 16), (0, 10, 20)
+LAT, PE = 80, 0.52
+TRY, ROUNDS = ((50, 1.0), (120, 1.4)), 1000
+B = 2.0 ** 40
+SB, LB, RB, ZC = 352, 648, 688, 720
+
+f32, bf, f16, i32, u16 = "float32", "bfloat16", "float16", "int32", "uint16"
+_S = {
+    i32: "xi 16 vi 16 wi 16 li 4 rows 256 seg 640 kraw 128 pi 8 lo 16 xpi 16",
+    bf: "ktab 128 pa 128 grow 128 cv 132 blk 128 blkh 128 ident 128 ir0 128 ni 128 l1 128 r1 128 t1 128 t2 128 sn 128 "
+        "sp 128 d0a 32 d0b 60 adj 320 adjl 128 sg 16 q2 32 tot 16 land0 8 cellb 16 rh 2112 hb 256 mask 320 kk 320 "
+        "aa 320 fl 60 fs 60 g1 20 fq 32",
+    f16: "identh 128 lpay 128 l20 128 l21 128 loe 160 cc 320",
+    u16: "jt16 16 cello 16 offe 8 uo16 20 xo16 20 off 40 dst 20 o16 16",
+    f32: "jraw 20 jidx 20 tv 24 col 40 e16 16 bb 8 tmp 48 mb16 256 mb8 192 jt 16 identf 128 inr1 128 sel0 128 sel1 128 "
+         "d0c 48 d0d 80 cr1 48 cr2 80 c64 4 al 16 qf 16 v64 16 nqc 16 xmb 16 y0 16 y1 20 thl 20 thr 20 thg 20 zz 20 "
+         "tt 136 eg 256 se 256 ve0 16 stat 256 pay 320 a0 80 a1 80 b0 80 b1 80 b2 64 xo 4 sc 160 sx 320 mx 80 junk 48 "
+         "win1 336 land1 72 landx 4 win2 728 xpb 16 uon 16 al2 16 al1 16 hc 16 c127 20 sin 128 ii 24 oo 64 res 256",
+}
+SCRATCH = {n: ("sbuf", [128, int(w)], d) for d, t in _S.items() for n, w in zip(t.split()[0::2], t.split()[1::2])}
+for _k in ("py0", "py1", "pu0", "pu1", "pp", "pt", "pr", "pm"):
+    SCRATCH[_k] = ("psum", [128, 512], f32)
+
+SEMAPHORES = ["sv", "ss", "sp", "sg", "ls", "x1", "x2", "x3"] + ["d%d" % i for i in range(12)]
+
+(RF, G16, NF, SGN, BQ, BQ1, PAYB, MKB, NR1, P8, M8, NB8, C40, C41, N8B, B127, R8, IB64, R16, PC, CC, EC, P9, M9, PB0,
+ NS) = range(26)
+
+
+def rank_program(g, core, T, topo):
+    rank = T.rank_of(core)
+    if rank is None:
+        return
+    cores = list(T.cores)
+    N = len(cores)
+    left, right = cores[(rank - 1) % N], cores[(rank + 1) % N]
+    sem = T.sem
+    Q = {"v": g.vector, "s": g.scalar, "p": g.tensor, "g": g, "y": g.sync}
+    own = {"v": "sv", "s": "ss", "p": "sp", "g": "sg"}
+    ops, wr, rd, bank, issue = [], {}, {}, {}, [1900]
+
+    def add(e, fn, hold, lat, r=(), w=(), b=None, kind="op"):
+        dep = {}
+        for n in r:
+            if n in wr:
+                dep[wr[n]] = True
+        for n in w:
+            for d in ([wr[n]] if n in wr else []) + rd.get(n, []):
+                dep[d] = True
+        if b in bank:
+            d = bank[b]
+            dep[d] = dep.get(d, False) or ops[d]["e"] != e
+        i = len(ops)
+        ops.append({"e": e, "fn": fn, "hold": hold, "lat": lat, "dep": dep, "kind": kind})
+        for n in r:
+            rd.setdefault(n, []).append(i)
+        for n in w:
+            wr[n] = i
+            rd[n] = []
+        if b is not None:
+            bank[b] = i
+
+    def vop(fn, n, r, w, b):
+        t = max(64, n) * 1.04
+        add("v", fn, t, t, r, w, b)
+
+    def ts(out, in0, s1, o0, s2=None, o1=None, r=(), w=(), b=None, n=0):
+        if o1 is None:
+            vop(lambda: g.vector.tensor_scalar(out, in0, s1, None, o0), n, r, w, b)
+        else:
+            vop(lambda: g.vector.tensor_scalar(out, in0, s1, s2, o0, o1), n, r, w, b)
+
+    def tt(out, in0, in1, o, r=(), w=(), b=None, n=0):
+        vop(lambda: g.vector.tensor_tensor(out, in0, in1, o), n, r, w, b)
+
+    def cp(out, in_, r=(), w=(), b=None, n=0):
+        vop(lambda: g.vector.tensor_copy(out, in_), n, r, w, b)
+
+    def scan(out, d0, d1, o0, o1, r=(), w=(), b=None, n=0):
+        vop(lambda: g.vector.tensor_tensor_scan(out, d0, d1, 0.0, o0, o1), n, r, w, b)
+
+    def act(out, in_, scale=1.0, bias=0.0, func=F.Identity, acc=None, r=(), w=(), b=None, n=0):
+        t = max(64, n) * 1.04 + 15
+        add("s", lambda: g.scalar.activation(out, in_, func, bias=bias, scale=scale, accum_out=acc), t, t, r, w, b)
+
+    def mm(out, lhsT, rhs, start, stop, r, b, n=64):
+        add("p", lambda: g.tensor.matmul(out, lhsT, rhs, start, stop), n * PE, n * PE, r, (), b)
+
+    def iota(out, pattern, base, mult, w, integer=False):
+        n = 1
+        for _, m in pattern:
+            n *= m
+        t = 165 + 2.1 * n
+        if integer:
+            add("g", lambda: g.iota(out, pattern, base, mult), t, t, (), w)
+        else:
+            add("g", lambda: g.iota(out, pattern, base, mult, allow_small_or_imprecise_dtypes=True), t, t, (), w)
+
+    def dma(e, out, in_, r=(), w=(), lat=1900):
+        add(e, lambda: Q[e].dma_start(out, in_), 60, lat, r, w, None, "dma")
+
+    def send(items, s, r, w):
+        trs = []
+        for src, dd, engs in items:
+            ids = [DstId(rid=topo.addr(d)[0], pnc=topo.addr(d)[1]) for d, _ in dd]
+            trs.append(RemoteDMATransfer(dst_ids=ids, dma_engine_mask=sum(1 << e for e in engs), remote_sem=sem[s],
+                                         srcs=[src], dsts=[o for _, o in dd]))
+        add("g", (trs, sum(len(x[2]) for x in items)), issue[0], issue[0], r, w, None, "send")
+        issue[0] = 400
+
+    def arrive(key, s, n, after, lat):
+        add(None, (s, n), 0, lat, after, [key], None, "arrive")
+
+    def gat(n):
+        return 60 + 1.56 * n
+
+    def c(i):
+        return T.col[:, i:i + 1]
+
+    def k(i):
+        return "c%d" % i
+
+    eng = topo.engines(core, right)
+    ne = len(eng)
+    half = ne // 2
+    B8, B16, IB8, IB16 = T.bb[:, 2:3], T.bb[:, 3:4], T.bb[:, 4:5], T.bb[:, 5:6]
+    I0, I1, I3, I4 = T.ii[:, 0:4], T.ii[:, 4:8], T.ii[:, 12:16], T.ii[:, 16:20]
+    O0, O1, O2, O3 = T.oo[:, 0:16], T.oo[:, 16:32], T.oo[:, 32:48], T.oo[:, 48:64]
+    MR, PCOL, ANY = T.cv[:, 0:128], T.jraw[:, 0:1], T.cv[:, 0:32]
+    E0, E1 = T.e16[:, 0:1], T.e16[:, 1:2]
+
+    dma("y", T.wi[:], T.w[:], w=["wi"])
+    dma("s", T.li[:, 0:1], T.live[:], w=["li"])
+    dma("y", T.xi[:], T.x[:], w=["xi"])
+    dma("s", T.seg[:, 64:576], T.med[:], w=["segm"], lat=3000)
+    vop(lambda: g.vector.memset(T.rows[:], 0), 256, (), ["rows"], None)
+    dma("y", T.rows[0::16, :], T.x[:], r=["rows"], w=["rowx"])
+    dma("y", T.rows[2::16, :], T.w[:], r=["rows"], w=["roww"])
+    dma("y", T.vi[:], T.v[:], w=["vi"])
+    dma("y", T.kraw[:], T.kick[:], w=["kraw"], lat=2200)
+
+    iota(T.pi[:, 0:1], [[0, 1]], 0, 1, ["pi"], True)
+    iota(T.jraw[:], [[16, 20]], 128, 1, ["jraw"])
+    for out, pat, base, w in (
+            (T.tv[:], [[1, 24]], -3, ["tv"]), (T.grow[:], [[16, 8], [0, 16]], 128, ["grow"]),
+            (T.d0a[:], [[0, 2], [64, 16]], 0, ["d0a"]), (MR, [[1, 128]], 128, ["cv0"]),
+            (T.b1[:], [[0, 20], [1000, 4]], -1873, ["b1"]), (T.b0[:], [[0, 20], [-10000, 4]], 20000, ["b0"]),
+            (T.a1[:], [[0, 20], [1000, 4]], -1873, ["a1", "ve", "vel", "ver"]), (T.a1[:, 1:64:4], [[0, 16]], 1, ["a1"]),
+            (T.a1[:, 65:80:4], [[0, 4]], -10000, ["a1"]), (T.a0[:], [[0, 80]], -30000, ["a0"]),
+            (T.win1[:], [[0, 336]], 0, ["win1", "fx"]), (T.d0c[:], [[0, 16], [10000, 3]], 0, ["d0c"]),
+            (T.cr1[:, 1::3], [[0, 16]], -1025, ["cr1b"]), (T.cr1[:, 2::3], [[0, 16]], 288 - 1025, ["cr1c"]),
+            (T.c64[:], [[0, 4]], 64, ["c64"]), (T.adjl[:, 0:64], [[0, 64]], 0, ["adjk"]),
+            (T.adjl[:, 64:128], [[8704, 2], [0, 32]], -8192, ["adjl"]),
+            (T.c127[:, 16:20], [[1, 2], [0, 2]], -1 if rank == N - 1 else 0, ["c127b"]),
+            (T.adj[:, 0:256], [[0, 256]], 0, ["adja"]), (T.adj[:, 256:320], [[16384, 2], [0, 32]], -8192, ["adjb"]),
+            (T.win2[:, 0:320], [[0, 320]], 0, ["win2"]), (T.win2[:, 320:LB], [[0, LB - 320]], 0, ["win2b", "cnt"]),
+            (T.win2[:, ZC:728], [[0, 8]], 0, ["zc"]), (T.d0b[:], [[0, 3], [64, 20]], 0, ["d0b"]),
+            (T.d0d[:], [[0, 20], [10000, 4]], 0, ["d0d"]), (T.cr2[:, 1::4], [[0, 20]], 320 - 1025, ["cr2b"]),
+            (T.cr2[:, 2::4], [[0, 20]], SB - 1025, ["cr2c"]), (T.cr2[:, 3::4], [[0, 20]], 608 - 1025, ["cr2d"])):
+        iota(out, pat, base, 0, w)
+
+    TR = ["tv", k(RF)]
+    ts(T.pi[:, 1:2], T.pi[:, 0:1], 15, A.bitwise_and, r=["pi"], w=["ri"])
+    ts(T.pi[:, 2:3], T.pi[:, 0:1], 1, A.bitwise_and, r=["pi"], w=["par"])
+    cp(c(RF), T.pi[:, 1:2], r=["ri"], w=[k(RF)])
+    ts(c(SGN), T.pi[:, 2:3], -256.0, A.mult, 128.0, A.add, r=["par"], w=[k(SGN)])
+    ts(c(G16), PCOL, c(RF), A.subtract, r=["jraw", k(RF)], w=[k(G16)])
+    ts(T.tmp[:, 0:16], T.tv[:, 2:18], c(RF), A.is_ge, B, A.mult, r=TR, w=["tm0"])
+    ts(T.tmp[:, 16:32], T.tv[:, 1:17], c(RF), A.is_lt, 1.0 / B, A.max, r=TR, w=["tm1"])
+    ts(T.tmp[:, 32:40], T.tv[:, 2:18:2], c(RF), A.is_ge, B, A.mult, r=TR, w=["tm2"])
+    ts(T.tmp[:, 40:48], T.tv[:, 0:16:2], c(RF), A.is_lt, 1.0 / B, A.max, r=TR, w=["tm3"])
+    tt(T.mb16[:, 0:16], T.tmp[:, 0:16], T.tmp[:, 16:32], A.mult, r=["tm0", "tm1"], w=["mb16"])
+    tt(T.mb8[:, 0:8], T.tmp[:, 32:40], T.tmp[:, 40:48], A.mult, r=["tm2", "tm3"], w=["mb8"])
+    ts(T.e16[:], T.tv[:, 3:19], c(RF), A.is_equal, r=TR, w=["e16"])
+    ts(T.bb[:, 0:2], T.tv[:, 17:19], c(RF), A.is_gt, B, A.mult, r=TR, w=["bb0"])
+    ts(T.bb[:, 4:6], T.tv[:, 17:19], c(RF), A.is_le, 1.0 / B, A.max, r=TR, w=["ib"])
+    ts(T.jidx[:], T.jraw[:], c(G16), A.subtract, r=["jraw", k(G16)], w=["jidx"])
+    ts(T.bb[:, 2:4], T.bb[:, 0:2], 1.0, A.max, r=["bb0"], w=["bb"])
+    ts(c(R16), c(RF), 16.0, A.mult, r=[k(RF)], w=[k(R16)])
+    ts(c(R8), c(RF), 7.5, A.is_gt, r=[k(RF)], w=[k(R8)])
+    ts(T.blk[:], T.grow[:], c(G16), A.is_equal, r=["grow", k(G16)], w=["blk"])
+    ts(T.jt[:], T.tv[:, 3:19], c(R16), A.add, r=["tv", k(R16)], w=["jt"])
+    ts(T.jt16[:], T.tv[:, 3:19], c(R16), A.add, r=["tv", k(R16)], w=["jt16"])
+    ts(T.offe[:], T.tv[:, 3:19:2], c(R8), A.add, r=["tv", k(R8)], w=["offe"])
+    ts(T.ident[:], MR, PCOL, A.is_equal, r=["cv0", "jraw"], w=["ident"])
+    ts(c(BQ), c(SGN), c(RF), A.mult, r=[k(SGN), k(RF)], w=[k(BQ)])
+    ts(c(BQ1), c(SGN), c(RF), A.mult, 128.0, A.add, r=[k(SGN), k(RF)], w=[k(BQ1)])
+    ts(T.l20[:, 0::2], T.blk[:, 0::2], 1.0, A.mult, r=["blk"], w=["l20a"])
+    ts(T.l20[:, 1::2], T.blk[:, 1::2], 0.0, A.mult, r=["blk"], w=["l20b"])
+    ts(T.l21[:, 0::2], T.blk[:, 0::2], 0.0, A.mult, r=["blk"], w=["l21a"])
+    ts(T.l21[:, 1::2], T.blk[:, 1::2], 1.0, A.mult, r=["blk"], w=["l21b"])
+    cp(T.identh[:], T.ident[:], r=["ident"], w=["identh"])
+    ts(T.t1[:], MR, c(G16), A.subtract, 1.5, A.is_le, r=["cv0", k(G16)], w=["t1"])
+    ts(T.t2[:], MR, PCOL, A.is_lt, -1.0, A.mult, r=["cv0", "jraw"], w=["t2"])
+    tt(T.lpay[:], T.t1[:], T.blk[:], A.mult, r=["t1", "blk"], w=["lpay"], n=256)
+    tt(T.t2[:], T.t2[:], T.blk[:], A.mult, r=["blk"], w=["t2"], n=256)
+
+    act(T.cv[:, 128:129], c(RF), 0.0, -1000.0, r=[k(RF)], w=["cv1"])
+    act(c(MKB), c(RF), -1.0, 192.0 - 255.5 / 512.0, r=[k(RF)], w=[k(MKB)])
+    for n0 in (16, 32, 64, 128):
+        act(T.mb16[:, n0:2 * n0], T.mb16[:, 0:n0], w=["mb16"], n=n0)
+        act(T.mb8[:, n0 // 2:n0], T.mb8[:, 0:n0 // 2], w=["mb8"])
+    act(T.mb8[:, 128:192], T.mb8[:, 0:64], w=["mb8"])
+    act(c(NR1), E1, -1.0, 1.0, r=["e16"], w=[k(NR1)])
+    for n, src, f, r in (("blkh", "blk", 0.5, []), ("sel0", "blk", E0, ["e16"]), ("sel1", "blk", E1, ["e16"]),
+                         ("ni", "ident", -1024.0, []), ("inr1", "ident", c(NR1), [k(NR1)]),
+                         ("ir0", "ident", E0, ["e16"]), ("identf", "ident", 1.0, [])):
+        act(T[n][:], T[src][:], f, r=[src] + r, w=[n], n=128)
+    act(T.sn[:, 0:127], T.ident[:, 1:128], r=["ident"], w=["sn"], n=128)
+    act(T.sp[:, 1:128], T.ident[:, 0:127], r=["ident"], w=["sp"], n=128)
+    act(T.sn[:, 15::16], T.ident[:, 0::16], r=["ident"], w=["sn"])
+    act(T.sp[:, 0::16], T.ident[:, 15::16], r=["ident"], w=["sp"])
+    act(T.l1[:, 0::2], T.blk[:, 0::2], 128.0, r=["blk"], w=["l1a"])
+    act(T.l1[:, 1::2], T.blk[:, 1::2], -128.0, r=["blk"], w=["l1b"])
+    tt(T.r1[:], T.t2[:], T.ni[:], A.subtract, r=["t2", "ni"], w=["r1"], n=256)
+    for i, src, f in ((NB8, B8, -1.0), (C40, B8, -4032.0), (C41, B8, 4160.0), (N8B, B8, 8192.0), (B127, B16, 127.0)):
+        act(c(i), src, f, r=["bb"], w=[k(i)])
+    for i, f in ((P9, 8492.0), (M9, -212.0), (P8, 8192.0), (M8, -8192.0), (PB0, -64.0)):
+        act(c(i), E0, f, r=["e16"], w=[k(i)])
+    act(c(PAYB), E1, -64.0, c(PB0), r=["e16", k(PB0)], w=[k(PAYB)])
+    act(c(IB64), IB8, 1.0 / 64, r=["ib"], w=[k(IB64)])
+    act(T.cr1[:, 0::3], T.jidx[:, 0:16], bias=32.0, r=["jidx"], w=["cr1a"])
+    act(T.cr2[:, 0::4], T.jidx[:], r=["jidx"], w=["cr2a"])
+    act(T.mask[:, 256:288], ANY, 0.0, E0, r=["cv0", "e16"], w=["maskl"])
+    act(T.mask[:, 288:320], ANY, 0.0, T.e16[:, 15:16], r=["cv0", "e16"], w=["maskr"])
+    act(T.win1[:, 8:40], ANY, 0.0, c(P9), r=["cv0", k(P9)], w=["win1"])
+    act(T.win1[:, 296:328], ANY, 0.0, c(M9), r=["cv0", k(M9)], w=["win1"])
+    act(T.win2[:, 320:352], ANY, 0.0, c(M8), r=["cv0", k(M8)], w=["win2b"])
+    act(T.win2[:, 608:640], ANY, 0.0, c(P8), r=["cv0", k(P8)], w=["win2b"])
+
+    cp(c(NF), T.li[:, 0:1], r=["li"], w=[k(NF)])
+    ts(T.sg[:], T.wi[:], -1.0, A.max, 1.0, A.min, r=["wi"], w=["sg"])
+    ts(T.al[:], T.jidx[:, 0:16], c(NF), A.is_lt, r=["jidx", k(NF)], w=["al"])
+    ts(T.cellb[:], T.xi[:], 1.0 / 64, A.mult, 128.0 - 31.5 / 64, A.add, r=["xi"], w=["cellb"])
+    tt(T.q2[:, 0:16], T.sg[:], T.al[:], A.mult, r=["sg", "al"], w=["q"])
+    tt(T.qf[:], T.sg[:], T.al[:], A.mult, r=["sg", "al"], w=["qf"])
+    act(T.q2[:, 16:32], T.q2[:, 0:16], r=["q"], w=["qb"])
+    if rank < N - 1:
+        scan(T.tot[:], T.d0a[:, 0:16], T.q2[:, 0:16], A.min, A.add, r=["d0a", "q"], w=["tot"])
+        send([(T.tot[:, 15:16], [(cores[d], T.land0[:, rank:rank + 1]) for d in range(N - 1, rank, -1)], eng)],
+             "x1", ["tot"], ["sent1"])
+    arrive("land0", "x1", ne * rank, ["q", "sent1"], 2800 if rank < N - 1 else 4700)
+
+    def field(ns, src, key):
+        ts(T.hc[:], T.cellb[:], -1.0, A.mult, 0.5, A.add, r=["cellb"], w=["hc"])
+        tt(T.nqc[:], T.qf[:], T.hc[:], A.mult, r=["qf", "hc"], w=["nqc"])
+        ts(T.cello[:], T.cellb[:], -128.0, A.add, 127.0, A.min, r=["cellb"], w=["cello"])
+        vs, ss_ = list(range(16 - ns)), list(range(16 - ns, 16))
+        order = []
+        if ns > 8:
+            order, ss_ = ss_[:ns - 2], ss_[ns - 2:]
+        while vs or ss_:
+            order += vs[:2] + ss_[:1]
+            vs, ss_ = vs[2:], ss_[1:]
+        for i, j in enumerate(order):
+            h = j >= 16 - ns
+            o = T.rh[:, 132 * j:132 * j + 129]
+            if h:
+                act(o, T.cv[:, 0:129], T.qf[:, j:j + 1], T.nqc[:, j:j + 1], F.Sign, r=["cv0", "cv1", "qf", "nqc"],
+                    w=["rh%d" % j], n=129)
+            else:
+                ts(o, T.cv[:, 0:129], T.cellb[:, j:j + 1], A.is_ge, T.q2[:, j:j + 1], A.mult,
+                   r=["cv0", "cv1", "cellb", "q"], w=["rh%d" % j])
+            mm(T.pt[:, 0:129], T.blkh[:] if h else T.blk[:], o, i == 0, i == 15, ["rh%d" % j, "blkh", "blk"], "pt", 129)
+        act(T.tt[:, 0:129], T.pt[:, 0:129], w=["tt"], b="pt", n=129)
+        act(T.eg[:], T.tt[:, 0:128].indirect(T.cello[:]), r=["tt", "cello"], w=["eg"], n=gat(256))
+        scan(T.se[:], T.mb16[:], T.eg[:], A.mult, A.add, r=["mb16", "eg"], w=["se"], n=256)
+        mm(T.pm[:, 0:256], T.sel0[:], src, True, True, [key, "sel0"], "pm", 1024)
+        act(T.hb[:], T.pm[:, 0:256], 1.0 / 512, c(MKB), r=[k(MKB)], w=["hb"], b="pm", n=256)
+        ts(T.mask[:, 0:256], T.hb[:], 192.0, A.is_equal, r=["hb"], w=["mask"], n=128)
+
+    def places(xint, key):
+        ts(T.lo[:], xint, 511, A.bitwise_and, r=[key], w=["lo"])
+        cp(T.loe[:, 0:128], T.lo[:].indirect(T.offe[:]), r=["lo", "offe"], w=["loe"], n=gat(128))
+        cp(T.b0[:, 3:64:4], T.lo[:], r=["lo"], w=["b0"])
+        ts(T.y0[:], xint, -4096.0, A.add, r=[key], w=["y0"])
+
+    def limits(a, e, r, w):
+        act(T.thl[:, a:e], T.y1[:, a:e], c(NB8), c(C40), r=r + [k(NB8), k(C40)], w=["thl" + w])
+        act(T.thr[:, a:e], T.y1[:, a:e], c(NB8), c(C41), r=r + [k(NB8), k(C41)], w=["thr" + w])
+
+    def first():
+        scan(T.b2[:], T.b0[:, 0:64], T.b1[:, 0:64], A.add, A.min, r=["b0", "b1"], w=["b2"])
+        cp(T.uo16[:, 0:16], T.b2[:, 2::4], r=["b2"], w=["uo16"])
+        cp(T.xo16[:, 0:16], T.b2[:, 3::4], r=["b2"], w=["xo16"])
+
+    cp(T.stat[:], T.rows[:].indirect(T.jt16[:]), r=["rows", "rowx", "roww", "jt16"], w=["stat"], n=gat(256))
+    field(NS1, T.stat[:], "stat")
+    cp(T.pa[:, 0:64], T.seg[:, 64:128], r=["segm"], w=["pa0"])
+    cp(T.pa[:, 64:128], T.seg[:, 512:576], r=["segm"], w=["pa1"])
+    mm(T.pu0[:, 0:64], T.sn[:], T.pa[:, 0:64], True, True, ["sn", "pa0"], "pu0")
+    mm(T.pu0[:, 64:128], T.sp[:], T.pa[:, 64:128], True, True, ["sp", "pa1"], "pu0")
+    cp(T.seg[:, 576:640], T.pu0[:, 0:64], w=["segr"], b="pu0")
+    cp(T.seg[:, 0:64], T.pu0[:, 64:128], w=["segl"], b="pu0")
+    ts(T.ktab[:], T.kraw[:], 64.0, A.add, r=["kraw"], w=["ktab"], n=128)
+    ts(T.v64[:], T.vi[:], 64.0, A.add, r=["vi"], w=["v64"])
+    places(T.xi[:], "xi")
+    ts(T.ve0[:], T.se[:, 15::16], IB16, A.mult, T.tt[:, 128:129], A.subtract, r=["se", "ib", "tt"], w=["ve0"])
+    tt(T.a1[:, 0:64:4], T.ve0[:], T.v64[:], A.add, r=["ve0", "v64"], w=["ve"])
+    mm(T.pp[:, 0:256], T.inr1[:], T.stat[:], True, False, ["inr1", "stat"], "pp", 1024)
+    tt(T.y1[:, 0:16], T.y0[:], T.al[:], A.mult, r=["y0", "al"], w=["y1"])
+    limits(0, 16, ["y1"], "")
+    ts(T.xmb[:], T.xi[:], -64.0, A.add, B8, A.mult, r=["xi", "bb"], w=["xmb"])
+
+    if rank > 0:
+        for d in range(rank):
+            mm(T.pr[:, 0:1], T.blk[:], T.land0[:, d:d + 1], d == 0, d == rank - 1, ["blk", "land0"], "pr")
+        ts(T.b1[:, 1:64:4], T.a1[:, 0:64:4], T.pr[:, 0:1], A.add, 1.0, A.max, r=["ve"], w=["b1"], b="pr")
+        act(c(PC), T.pr[:, 0:1], w=[k(PC)], b="pr")
+    else:
+        ts(T.b1[:, 1:64:4], T.a1[:, 0:64:4], 1.0, A.max, r=["ve", "land0"], w=["b1"])
+    first()
+    mm(T.pr[:, 0:48], T.identf[:], T.cr1[:], True, False, ["identf", "cr1a", "cr1b", "cr1c"], "pr", 256)
+
+    def scatterings(cut):
+        nch = len(cut) - 1
+        names = ("py0", "py1", "pu0", "pu1")
+        for i in range(3):
+            for h in range(nch):
+                a, e = cut[h], cut[h + 1]
+                n = 8 * (e - a)
+                m1, m2 = max(64, n), max(64, 2 * n)
+                inc = e > 16
+                yb, ub = (names[h], names[h + 2]) if nch == 2 else (names[h], names[h])
+                u0 = 0 if nch == 2 else 256
+                PY, PU = T[yb], T[ub]
+                kk, aa, ck, ok = "kk%d" % h, "aa%d" % h, "cc%d" % h, "off%d" % h
+                K, AA, CC_ = T.kk[:, 16 * a:16 * e], T.aa[:, 16 * a:16 * e], T.cc[:, 16 * a:16 * e]
+                ev, od = T.cc[:, 16 * a:16 * e:2], T.cc[:, 16 * a + 1:16 * e:2]
+                if i == 0:
+                    ou, ox = T.uo16[:, a:e], T.xo16[:, a:e]
+                    ru, rx = ["uo16"] + ["uoi"] * inc, ["xo16"] + ["xoi"] * inc
+                else:
+                    ou, ox, ru, rx = T.off[:, 2 * a:a + e], T.off[:, a + e:2 * e], [ok], [ok]
+                act(K, T.ktab[:].indirect(ou), r=["ktab"] + ru, w=[kk], n=gat(2 * n))
+                tt(AA, T.seg[:].indirect(ox), T.mask[:, 16 * a:16 * e], A.mult,
+                   r=["segm", "segl", "segr", "mask", "maskl", "maskr"] + rx, w=[aa], n=gat(2 * n))
+                mm(PY[:, 0:2 * n], T.ident[:], K, True, False, ["ident", kk], yb, m2)
+                mm(PY[:, 0:2 * n], T.l1[:], AA, False, True, ["l1a", "l1b", aa], yb, m2)
+                lo_mm = (PU[:, u0 + n:u0 + 2 * n], T.identh[:], T.loe[:, 8 * a:8 * e], True, False,
+                         ["identh", "loe"] + ["loi"] * inc, ub, m1)
+                if i < 2 and nch == 2:
+                    mm(*lo_mm)
+                ts(CC_, PY[:, 0:2 * n], c(BQ), A.max, c(BQ1), A.min, r=[k(BQ), k(BQ1)], w=[ck], b=yb, n=2 * n)
+                if i < 2:
+                    if nch > 2:
+                        mm(*lo_mm)
+                    mm(PU[:, u0 + n:u0 + 2 * n], T.l20[:], ev, False, False, ["l20a", "l20b", ck], ub, m1)
+                    mm(PU[:, u0 + n:u0 + 2 * n], T.l21[:], od, False, True, ["l21a", "l21b", ck], ub, m1)
+                mm(PU[:, u0:u0 + n], T.l20[:], ev, True, False, ["l20a", "l20b", ck], ub, m1)
+                mm(PU[:, u0:u0 + n], T.l21[:], od, False, True, ["l21a", "l21b", ck], ub, m1)
+                if i == 2:
+                    mm(T.pp[:, 16 * a:16 * e], T.lpay[:], CC_, False, h == nch - 1, ["lpay", ck], "pp", m2)
+                    scan(T.sc[:, 8 * a:8 * e], T.mb8[:, 0:n], PU[:, u0:u0 + n], A.mult, A.add, r=["mb8"],
+                         w=["sc%d" % h], b=ub, n=n)
+                else:
+                    scan(T.sx[:, 16 * a:16 * e], T.mb8[:, 0:2 * n], PU[:, u0:u0 + 2 * n], A.mult, A.add, r=["mb8"],
+                         w=["sx%d" % h], b=ub, n=2 * n)
+                    ts(T.off[:, 2 * a:2 * e], T.sx[:, 16 * a + 7:16 * e:8], IB8, A.mult, r=["sx%d" % h, "ib"], w=[ok])
+        return ["sc%d" % h for h in range(nch)]
+
+    SC = scatterings(CUT1)
+
+    U = T.sc[:, 7:128:8]
+    act(T.pay[:, 0:256], T.pp[:, 0:256], 1.0, c(PAYB), r=[k(PAYB)], w=["pay"], b="pp", n=256)
+    tt(T.fl[:, 0:16], U, T.thr[:, 0:16], A.is_ge, r=SC + ["thr"], w=["fr"])
+    tt(T.fl[:, 16:32], U, T.thl[:, 0:16], A.is_lt, r=SC + ["thl"], w=["fl"])
+    tt(T.xpb[:], U, T.xmb[:], A.add, r=SC + ["xmb"], w=["xpb"])
+    scan(T.fs[:, 0:32], T.d0a[:], T.fl[:, 0:32], A.min, A.add, r=["d0a", "fr", "fl"], w=["fs"])
+    mm(T.pr[:, 1:48:3], T.r1[:], T.fl[:, 0:16], False, False, ["r1", "fr"], "pr")
+    mm(T.pr[:, 0:48:3], T.ni[:], T.fl[:, 0:16], False, False, ["ni", "fr"], "pr")
+    mm(T.pr[:, 2:48:3], T.r1[:], T.fl[:, 16:32], False, False, ["r1", "fl"], "pr")
+    mm(T.pr[:, 1:48:3], T.blk[:], T.fs[:, 0:16], False, False, ["blk", "fs"], "pr")
+    mm(T.pr[:, 2:48:3], T.blk[:], T.fs[:, 16:32], False, True, ["blk", "fs"], "pr")
+    scan(T.mx[:, 0:48], T.d0c[:], T.pr[:, 0:48], A.min, A.max, r=["d0c"], w=["mx"], b="pr")
+    cp(T.dst[:, 0:16], T.mx[:, 2:48:3], r=["mx"], w=["dst"])
+    cp(T.win1[:, 8:328].indirect(T.dst[:, 0:16]), T.pay[:, 0:256], r=["pay", "dst"], w=["win1"], n=60 + 3.8 * 256)
+    tt(T.fq[:], T.fl[:, 0:32], T.q2[:], A.mult, r=["fr", "fl", "q", "qb"], w=["fq"])
+    mm(T.pm[:, 0:32], T.blk[:], T.fq[:], True, True, ["blk", "fq"], "pm")
+    fluxes = [(1, 328)]
+    if rank == 0:
+        fluxes = [(1, 4), (1, 328)]
+    if rank == N - 1:
+        fluxes = [(0, 4), (1, 328), (0, 329)]
+    for i, (h, cidx) in enumerate(fluxes):
+        act(T.junk[:, 16 * i:16 * i + 16], T.pm[:, 16 * h:16 * h + 16], acc=T.win1[:, cidx:cidx + 1], r=["fx"],
+            w=["fx%d" % i], b="pm")
+    fx = ["fx%d" % i for i in range(len(fluxes))]
+    if rank in (0, N - 1):
+        send([(T.win1[:, 4:5], [(cores[(rank + 2) % N], T.landx[:, 0:1])], eng)], "x2", ["fx0"], ["sentx"])
+        arrive("landx", "x2", 0, ["sentx"], 2400)
+    send([(T.win1[:, 4:40], [(right, T.land1[:, 0:36])], eng[:half]),
+          (T.win1[:, 296:332], [(left, T.land1[:, 36:72])], eng[half:])], "x2", ["win1", "sentx"] + fx, ["sent2"])
+    arrive("land1", "x2", ne if rank in (0, N - 1) else 2 * ne, ["sent2"], 2800)
+
+    ts(T.cellb[:], T.xpb[:], c(IB64), A.mult, 128.0 - 31.5 / 64, A.add, r=["xpb", k(IB64)], w=["cellb"])
+    ts(T.xpi[:], T.xpb[:], IB8, A.mult, r=["xpb", "ib"], w=["xpi"])
+    field(NS2, T.pay[:, 0:256], "pay")
+    places(T.xpi[:], "xpi")
+    ts(T.uon[:], U, IB8, A.mult, r=SC + ["ib"], w=["uon"])
+    if rank == N - 1:
+        ts(T.c127[:, 0:16], T.cellb[:], 255.0, A.is_equal, -1.0, A.add, r=["cellb"], w=["c127a"])
+    else:
+        ts(T.c127[:, 0:16], T.cellb[:], 255.0, A.is_equal, r=["cellb"], w=["c127a"])
+    tt(T.al1[:], T.al[:], T.fl[:, 0:16], A.subtract, r=["al", "fr"], w=["al1"])
+    tt(T.al2[:], T.al1[:], T.fl[:, 16:32], A.subtract, r=["al1", "fl"], w=["al2"])
+    ts(T.zz[:, 0:16], T.al2[:], 0.5, A.is_lt, c(N8B), A.mult, r=["al2", k(N8B)], w=["zz"])
+    tt(T.y1[:, 0:16], T.y0[:], T.al2[:], A.mult, r=["y0", "al2"], w=["y1"])
+    limits(0, 16, ["y1"], "")
+    tt(T.thg[:, 0:16], T.thl[:, 0:16], T.zz[:, 0:16], A.add, r=["thl", "zz"], w=["thg"])
+    mm(T.pp[:, 0:320], T.ir0[:], T.adj[:], True, False, ["ir0", "adja", "adjb"], "pp", 320)
+    mm(T.pp[:, 0:256], T.inr1[:], T.pay[:, 0:256], False, False, ["inr1", "pay"], "pp", 1024)
+    mm(T.pr[:, 0:80], T.identf[:], T.cr2[:], True, False, ["identf", "cr2a", "cr2b", "cr2c", "cr2d"], "pr", 320)
+    TX = T.tt[:, 128:129]
+    if rank == 0:
+        ts(c(CC), TX, -1.0, A.mult, T.win1[:, 328:329], A.subtract, r=["tt"] + fx, w=[k(CC)])
+    elif rank == N - 1:
+        ts(c(CC), c(PC), TX, A.subtract, T.win1[:, 329:330], A.add, r=["tt", k(PC)] + fx, w=[k(CC)])
+    else:
+        ts(c(CC), c(PC), TX, A.subtract, r=["tt", k(PC)], w=[k(CC)])
+    ts(T.a1[:, 64:72:4], T.c64[:, 0:2], T.tt[:, 0:1], A.add, c(CC), A.add, r=["c64", "tt", k(CC)], w=["vel"])
+    ts(T.a1[:, 72:80:4], T.c64[:, 0:2], T.tt[:, 127:128], A.add, c(CC), A.add, r=["c64", "tt", k(CC)], w=["ver"])
+    ts(T.ve0[:], T.se[:, 15::16], IB16, A.mult, c(CC), A.add, r=["se", k(CC)], w=["ve0"])
+    tt(T.a1[:, 0:64:4], T.ve0[:], T.uon[:], A.add, r=["ve0", "uon"], w=["ve"])
+
+    mm(T.pm[:, 0:128], T.ident[:], T.adjl[:], True, False, ["ident", "adjk", "adjl"], "pm", 128)
+    mm(T.pm[:, 0:64], T.sel1[:], T.land1[:, 4:68], False, False, ["sel1", "land1"], "pm", 256)
+    mm(T.pm[:, 64:128], T.sel0[:], T.land1[:, 4:68], False, True, ["sel0", "land1"], "pm", 256)
+    mm(T.pp[:, 256:320], T.inr1[:], T.land1[:, 4:68], False, False, ["inr1", "land1"], "pp", 256)
+    VE = ["ve", "vel", "ver"]
+    C127 = ["c127a", "c127b", "land1", "landx"]
+    inr = T.land1[:, 68:69]
+    if rank == N - 1:
+        ts(T.a0[:, 1::4], T.c127[:], inr, A.mult, r=C127, w=["a0"])
+    else:
+        r3 = (T.land1[:, 0:1], T.landx[:, 0:1], T.land1[:, 69:70])[rank]
+        ts(T.a0[:, 1::4], T.c127[:], inr, A.mult, r3, A.add, r=C127, w=["a0"])
+    if rank not in (0, N - 1):
+        l0 = T.land1[:, 0:1] if rank == 1 else T.landx[:, 0:1]
+        ts(T.a1[:, 0::4], T.a1[:, 0::4], l0, A.subtract, r=["land1"], w=VE)
+    scan(T.b1[:], T.a0[:], T.a1[:], A.add, A.max, r=["a0", "a1"] + VE, w=["b1"], n=80)
+    first()
+    scan(T.sin[:], T.mb16[:, 0:128], T.pm[:, 0:128], A.mult, A.add, r=["mb16"], w=["sin"], b="pm", n=128)
+    I2 = T.sin[:, 79:128:16]
+    act(I0, T.b1[:, 65:80:4], B16, r=["b1", "bb"], w=["i0"])
+    act(I4, I2, IB16, r=["sin", "ib"], w=["i4"])
+    tt(I1, I0, T.sin[:, 15:64:16], A.add, r=["i0", "sin"], w=["i1"])
+    ts(I3, I1, B16, A.max, c(B127), A.min, r=["i1", k(B127)], w=["i3"])
+    tt(T.xo[:], I3, I2, A.add, r=["i3", "sin"], w=["xo"])
+    ts(T.uo16[:, 16:20], I3, IB16, A.mult, r=["i3"], w=["uoi"])
+    ts(T.xo16[:, 16:20], T.xo[:], IB16, A.mult, r=["xo"], w=["xoi"])
+    cp(T.loe[:, 128:160], I4.indirect(T.offe[:, 0:2]), r=["i4", "offe"], w=["loi"], n=gat(32))
+    ts(T.zz[:, 16:20], I4, 300.0, A.is_equal, c(N8B), A.mult, r=["i4", k(N8B)], w=["zzi"])
+    act(T.y1[:, 16:18], T.ii[:, 16:18], 1.0, -4096.0, r=["i4"], w=["y0b"])
+    act(T.y1[:, 18:20], T.ii[:, 18:20], 1.0, 3584.0, r=["i4"], w=["y0c"])
+    limits(16, 20, ["y0b", "y0c"], "i")
+    tt(T.thg[:, 16:20], T.thl[:, 16:20], T.zz[:, 16:20], A.add, r=["thli", "zzi"], w=["thgi"])
+
+    SC = scatterings(CUT2)
+
+    U = T.sc[:, 7:160:8]
+    act(T.pay[:], T.pp[:, 0:320], 1.0, c(PAYB), w=["pay"], b="pp", n=320)
+    tt(T.fl[:, 40:60], U, T.thr[:], A.is_ge, r=SC + ["thr", "thri"], w=["f2"])
+    tt(T.g1[:], U, T.thg[:], A.is_ge, r=SC + ["thg", "thgi"], w=["g1"])
+    tt(T.fl[:, 0:20], U, T.thl[:], A.is_lt, r=SC + ["thl", "thli"], w=["f0", "fr", "fl"])
+    tt(T.fl[:, 20:40], T.g1[:], T.fl[:, 40:60], A.subtract, r=["g1", "f2"], w=["f1", "fl"])
+    scan(T.fs[:], T.d0b[:], T.fl[:], A.min, A.add, r=["d0b", "f0", "f1", "f2"], w=["fs"])
+    for j in (2, 0, 1):
+        mm(T.pr[:, j + 1:80:4], T.r1[:], T.fl[:, 20 * j:20 * j + 20], False, False, ["r1", "f%d" % j], "pr")
+    for j in range(3):
+        mm(T.pr[:, j + 1:80:4], T.blk[:], T.fs[:, 20 * j:20 * j + 20], False, j == 2, ["blk", "fs"], "pr")
+    mm(T.pm[:, 0:2], T.blk[:], T.fs[:, 39:60:20], True, True, ["blk", "fs"], "pm")
+    scan(T.mx[:], T.d0d[:], T.pr[:, 0:80], A.min, A.max, r=["d0d"], w=["mx"], b="pr", n=80)
+    act(T.win2[:, 640:641], T.pm[:, 1:2], 1.0, float(LB), r=["cnt"], w=["cn0"], b="pm")
+    act(T.win2[:, 641:642], T.pm[:, 1:2], -1.0, float(RB - LB), r=["cnt"], w=["cn1"], b="pm")
+    act(c(EC), T.pm[:, 0:1], -1.0, float(LB - SB), w=[k(EC)], b="pm")
+    act(c(NS), T.pm[:, 0:1], w=[k(NS)], b="pm")
+    cp(T.dst[:], T.mx[:, 3:80:4], r=["mx"], w=["dst"])
+    cp(T.win2[:, 0:640].indirect(T.dst[:]), T.pay[:], r=["pay", "dst"], w=["win2", "win2b"], n=60 + 3.8 * 320)
+    send([(T.win2[:, 608:644], [(right, T.win2[:, LB:LB + 36])], eng[:half]),
+          (T.win2[:, 316:352], [(left, T.win2[:, RB - 4:RB + 32])], eng[half:])], "x3", ["win2", "cn0", "cn1"],
+         ["sent3"])
+    arrive("land2", "x3", ne, ["sent3"], 2800)
+    ts(O0, T.jt[:], c(NS), A.is_ge, c(EC), A.mult, r=["jt", k(NS), k(EC)], w=["o0"])
+    ts(O1, T.jt[:], float(SB), A.add, r=["jt"], w=["o1"])
+    tt(O2, O0, O1, A.add, r=["o0", "o1"], w=["o2"])
+    ts(O0, O2, T.win2[:, LB + 32:LB + 33], A.is_ge, T.win2[:, LB + 33:LB + 34], A.mult, r=["o2", "land2"], w=["o0"])
+    act(T.win2[:, LB:LB + 32], T.win2[:, LB:LB + 32], 1.0, c(M8), r=["land2", k(M8)], w=["fixl"])
+    act(T.win2[:, RB:RB + 32], T.win2[:, RB:RB + 32], 1.0, c(P8), r=["land2", k(P8)], w=["fixr"])
+    tt(O3, O0, O2, A.add, r=["o0", "o2"], w=["o3"])
+    ts(T.o16[:], O3, float(ZC), A.min, r=["o3"], w=["o16"])
+    W2 = ["o16", "win2", "fixl", "fixr", "zc", "cn0", "cn1", "land2"]
+    cp(T.res[:, 0:128], T.win2[:].indirect(T.o16[:, 0:8]), r=W2, w=["res"], n=gat(128))
+    act(T.res[:, 128:256], T.win2[:].indirect(T.o16[:, 8:16]), r=W2, w=["res2"], n=gat(128))
+    dma("y", T.yx[:], T.res[0::16, :], r=["res", "res2"])
+    dma("s", T.yv[:], T.res[1::16, :], r=["res", "res2"])
+    dma("y", T.yw[:], T.res[2::16, :], r=["res", "res2"])
+
+    n_ops = len(ops)
+    deps = [list(o["dep"].items()) for o in ops]
+    users = [[] for _ in ops]
+    for i, dd in enumerate(deps):
+        for d, _ in dd:
+            users[d].append(i)
+    hold, late, where = [o["hold"] for o in ops], [o["lat"] for o in ops], [o["e"] for o in ops]
+
+    def place(prio):
+        todo = [len(dd) for dd in deps]
+        ready = [i for i in range(n_ops) if not todo[i]]
+        at, busy = [0.0] * n_ops, {e: [] for e in Q}
+        while ready:
+            i = max(ready, key=lambda x: prio[x])
+            ready.remove(i)
+            t = 0.0
+            for d, wait in deps[i]:
+                t = max(t, at[d] + late[d] + (LAT if wait else 0))
+            if where[i] is not None:
+                b, j = busy[where[i]], 0
+                while j < len(b) and t + hold[i] > b[j][0]:
+                    t = max(t, b[j][1])
+                    j += 1
+                b.insert(j, (t, t + hold[i]))
+            at[i] = t
+            for u in users[i]:
+                todo[u] -= 1
+                if not todo[u]:
+                    ready.append(u)
+        return sorted(range(n_ops), key=lambda x: (at[x], x))
+
+    def length(order):
+        total = 0.0
+        for lat, pe in TRY:
+            end, free = [0.0] * n_ops, {e: 0.0 for e in Q}
+            for i in order:
+                e = where[i]
+                t = free[e] if e else 0.0
+                for d, wait in deps[i]:
+                    if wait:
+                        t = max(t, end[d] + lat)
+                f = pe if e == "p" else 1.0
+                if e:
+                    free[e] = t + hold[i] * f
+                end[i] = t + late[i] * f
+            total += max(end)
+        return total
+
+    level = [0.0] * n_ops
+    for i in range(n_ops - 1, -1, -1):
+        level[i] += late[i]
+        for d, wait in deps[i]:
+            level[d] = max(level[d], level[i] + (LAT if wait else 0))
+    rng = np.random.default_rng(rank)
+    order = place(level)
+    best = length(order)
+    for turn in range(ROUNDS):
+        moved = list(level)
+        for i in rng.integers(0, n_ops, 6):
+            moved[int(i)] += float(rng.normal(0, 1)) * (300 if turn % 2 else 2500)
+        cand = place(moved)
+        size = length(cand)
+        if size <= best:
+            level, order, best = moved, cand, size
+    count, clock, tok = {}, {e: {} for e in Q}, {}
+    nd = 0
+    for i in order:
+        o = ops[i]
+        e = o["e"]
+        if e is None:
+            s, n = o["fn"]
+            if n:
+                count[s] = n
+                tok[i] = (s, n, {})
+            continue
+        for s, v, clk in sorted([tok[d] for d, wait in deps[i] if wait and d in tok], key=lambda x: -x[1]):
+            if clock[e].get(s, 0) < v:
+                Q[e].wait_ge(sem[s], v)
+                for n, x in clk.items():
+                    clock[e][n] = max(clock[e].get(n, 0), x)
+                clock[e][s] = v
+        if o["kind"] == "send":
+            g.remote_dma_fused(o["fn"][0], local_sem=sem.ls)
+            count["ls"] = count.get("ls", 0) + o["fn"][1]
+            continue
+        s, inc = (own[e], 1) if o["kind"] == "op" else ("d%d" % nd, 16)
+        nd += o["kind"] == "dma"
+        o["fn"]().then_inc(sem[s], inc)
+        count[s] = count.get(s, 0) + inc
+        tok[i] = (s, count[s], dict(clock[e]))
+    for s, n in count.items():
+        g.wait_ge(sem[s], n)

@@ -2,10 +2,10 @@ import numpy as np
 from concourse.bass import DstId, RemoteDMATransfer
 from concourse.mybir import AluOpType as A, ActivationFunctionType as F
 
-NS1, NS2 = 5, 12
-CUT1, CUT2 = (0, 8, 16), (0, 10, 20)
-LAT, PE = 80, 0.52
-TRY, ROUNDS = ((50, 1.0), (120, 1.4)), 1000
+NS1, NS2 = 5, 10
+CUT1, CUT2 = (0, 6, 12, 16), (0, 6, 14, 20)
+LAT, PE = 150, 0.52
+TRY, ROUNDS = ((100, 1.0), (180, 1.2)), 1500
 B = 2.0 ** 40
 SB, LB, RB, ZC = 352, 648, 688, 720
 
@@ -14,7 +14,7 @@ _S = {
     i32: "xi 16 vi 16 wi 16 li 4 rows 256 seg 640 kraw 128 pi 8 lo 16 xpi 16",
     bf: "ktab 128 pa 128 grow 128 cv 132 blk 128 blkh 128 ident 128 ir0 128 ni 128 l1 128 r1 128 t1 128 t2 128 sn 128 "
         "sp 128 d0a 32 d0b 60 adj 320 adjl 128 sg 16 q2 32 tot 16 land0 8 cellb 16 rh 2112 hb 256 mask 320 kk 320 "
-        "aa 320 fl 60 fs 60 g1 20 fq 32",
+        "aa 320 fl 60 fs 60 nt2 128 nblk 128 fq 32",
     f16: "identh 128 lpay 128 l20 128 l21 128 loe 160 cc 320",
     u16: "jt16 16 cello 16 offe 8 uo16 20 xo16 20 off 40 dst 20 o16 16",
     f32: "jraw 20 jidx 20 tv 24 col 40 e16 16 bb 8 tmp 48 mb16 256 mb8 192 jt 16 identf 128 inr1 128 sel0 128 sel1 128 "
@@ -205,11 +205,11 @@ def rank_program(g, core, T, topo):
     for n0 in (16, 32, 64, 128):
         act(T.mb16[:, n0:2 * n0], T.mb16[:, 0:n0], w=["mb16"], n=n0)
         act(T.mb8[:, n0 // 2:n0], T.mb8[:, 0:n0 // 2], w=["mb8"])
-    act(T.mb8[:, 128:192], T.mb8[:, 0:64], w=["mb8"])
     act(c(NR1), E1, -1.0, 1.0, r=["e16"], w=[k(NR1)])
     for n, src, f, r in (("blkh", "blk", 0.5, []), ("sel0", "blk", E0, ["e16"]), ("sel1", "blk", E1, ["e16"]),
                          ("ni", "ident", -1024.0, []), ("inr1", "ident", c(NR1), [k(NR1)]),
-                         ("ir0", "ident", E0, ["e16"]), ("identf", "ident", 1.0, [])):
+                         ("ir0", "ident", E0, ["e16"]), ("identf", "ident", 1.0, []), ("nt2", "t2", -1.0, []),
+                         ("nblk", "blk", -1.0, [])):
         act(T[n][:], T[src][:], f, r=[src] + r, w=[n], n=128)
     act(T.sn[:, 0:127], T.ident[:, 1:128], r=["ident"], w=["sn"], n=128)
     act(T.sp[:, 1:128], T.ident[:, 0:127], r=["ident"], w=["sp"], n=128)
@@ -319,15 +319,13 @@ def rank_program(g, core, T, topo):
 
     def scatterings(cut):
         nch = len(cut) - 1
-        names = ("py0", "py1", "pu0", "pu1")
         for i in range(3):
             for h in range(nch):
                 a, e = cut[h], cut[h + 1]
                 n = 8 * (e - a)
                 m1, m2 = max(64, n), max(64, 2 * n)
                 inc = e > 16
-                yb, ub = (names[h], names[h + 2]) if nch == 2 else (names[h], names[h])
-                u0 = 0 if nch == 2 else 256
+                yb, ub = ("py0", "py1", "pt")[h], ("pu0", "pu1", "pm")[h]
                 PY, PU = T[yb], T[ub]
                 kk, aa, ck, ok = "kk%d" % h, "aa%d" % h, "cc%d" % h, "off%d" % h
                 K, AA, CC_ = T.kk[:, 16 * a:16 * e], T.aa[:, 16 * a:16 * e], T.cc[:, 16 * a:16 * e]
@@ -342,24 +340,21 @@ def rank_program(g, core, T, topo):
                    r=["segm", "segl", "segr", "mask", "maskl", "maskr"] + rx, w=[aa], n=gat(2 * n))
                 mm(PY[:, 0:2 * n], T.ident[:], K, True, False, ["ident", kk], yb, m2)
                 mm(PY[:, 0:2 * n], T.l1[:], AA, False, True, ["l1a", "l1b", aa], yb, m2)
-                lo_mm = (PU[:, u0 + n:u0 + 2 * n], T.identh[:], T.loe[:, 8 * a:8 * e], True, False,
-                         ["identh", "loe"] + ["loi"] * inc, ub, m1)
-                if i < 2 and nch == 2:
-                    mm(*lo_mm)
+                if i < 2:
+                    mm(PU[:, n:2 * n], T.identh[:], T.loe[:, 8 * a:8 * e], True, False,
+                       ["identh", "loe"] + ["loi"] * inc, ub, m1)
                 ts(CC_, PY[:, 0:2 * n], c(BQ), A.max, c(BQ1), A.min, r=[k(BQ), k(BQ1)], w=[ck], b=yb, n=2 * n)
                 if i < 2:
-                    if nch > 2:
-                        mm(*lo_mm)
-                    mm(PU[:, u0 + n:u0 + 2 * n], T.l20[:], ev, False, False, ["l20a", "l20b", ck], ub, m1)
-                    mm(PU[:, u0 + n:u0 + 2 * n], T.l21[:], od, False, True, ["l21a", "l21b", ck], ub, m1)
-                mm(PU[:, u0:u0 + n], T.l20[:], ev, True, False, ["l20a", "l20b", ck], ub, m1)
-                mm(PU[:, u0:u0 + n], T.l21[:], od, False, True, ["l21a", "l21b", ck], ub, m1)
+                    mm(PU[:, n:2 * n], T.l20[:], ev, False, False, ["l20a", "l20b", ck], ub, m1)
+                    mm(PU[:, n:2 * n], T.l21[:], od, False, True, ["l21a", "l21b", ck], ub, m1)
+                mm(PU[:, 0:n], T.l20[:], ev, True, False, ["l20a", "l20b", ck], ub, m1)
+                mm(PU[:, 0:n], T.l21[:], od, False, True, ["l21a", "l21b", ck], ub, m1)
                 if i == 2:
                     mm(T.pp[:, 16 * a:16 * e], T.lpay[:], CC_, False, h == nch - 1, ["lpay", ck], "pp", m2)
-                    scan(T.sc[:, 8 * a:8 * e], T.mb8[:, 0:n], PU[:, u0:u0 + n], A.mult, A.add, r=["mb8"],
+                    scan(T.sc[:, 8 * a:8 * e], T.mb8[:, 0:n], PU[:, 0:n], A.mult, A.add, r=["mb8"],
                          w=["sc%d" % h], b=ub, n=n)
                 else:
-                    scan(T.sx[:, 16 * a:16 * e], T.mb8[:, 0:2 * n], PU[:, u0:u0 + 2 * n], A.mult, A.add, r=["mb8"],
+                    scan(T.sx[:, 16 * a:16 * e], T.mb8[:, 0:2 * n], PU[:, 0:2 * n], A.mult, A.add, r=["mb8"],
                          w=["sx%d" % h], b=ub, n=2 * n)
                     ts(T.off[:, 2 * a:2 * e], T.sx[:, 16 * a + 7:16 * e:8], IB8, A.mult, r=["sx%d" % h, "ib"], w=[ok])
         return ["sc%d" % h for h in range(nch)]
@@ -396,7 +391,7 @@ def rank_program(g, core, T, topo):
         arrive("landx", "x2", 0, ["sentx"], 2400)
     send([(T.win1[:, 4:40], [(right, T.land1[:, 0:36])], eng[:half]),
           (T.win1[:, 296:332], [(left, T.land1[:, 36:72])], eng[half:])], "x2", ["win1", "sentx"] + fx, ["sent2"])
-    arrive("land1", "x2", ne if rank in (0, N - 1) else 2 * ne, ["sent2"], 2800)
+    arrive("land1", "x2", ne if rank in (0, N - 1) else 2 * ne, ["sent2"], 2400)
 
     ts(T.cellb[:], T.xpb[:], c(IB64), A.mult, 128.0 - 31.5 / 64, A.add, r=["xpb", k(IB64)], w=["cellb"])
     ts(T.xpi[:], T.xpb[:], IB8, A.mult, r=["xpb", "ib"], w=["xpi"])
@@ -466,15 +461,17 @@ def rank_program(g, core, T, topo):
     U = T.sc[:, 7:160:8]
     act(T.pay[:], T.pp[:, 0:320], 1.0, c(PAYB), w=["pay"], b="pp", n=320)
     tt(T.fl[:, 40:60], U, T.thr[:], A.is_ge, r=SC + ["thr", "thri"], w=["f2"])
-    tt(T.g1[:], U, T.thg[:], A.is_ge, r=SC + ["thg", "thgi"], w=["g1"])
     tt(T.fl[:, 0:20], U, T.thl[:], A.is_lt, r=SC + ["thl", "thli"], w=["f0", "fr", "fl"])
-    tt(T.fl[:, 20:40], T.g1[:], T.fl[:, 40:60], A.subtract, r=["g1", "f2"], w=["f1", "fl"])
+    tt(T.fl[:, 20:40], U, T.thg[:], A.is_ge, r=SC + ["thg", "thgi", "al2", "fq"], w=["f1"])
     scan(T.fs[:], T.d0b[:], T.fl[:], A.min, A.add, r=["d0b", "f0", "f1", "f2"], w=["fs"])
     for j in (2, 0, 1):
         mm(T.pr[:, j + 1:80:4], T.r1[:], T.fl[:, 20 * j:20 * j + 20], False, False, ["r1", "f%d" % j], "pr")
+    mm(T.pr[:, 2:80:4], T.nt2[:], T.fl[:, 40:60], False, False, ["nt2", "f2"], "pr")
+    mm(T.pr[:, 2:80:4], T.nblk[:], T.fs[:, 40:60], False, False, ["nblk", "fs"], "pr")
     for j in range(3):
         mm(T.pr[:, j + 1:80:4], T.blk[:], T.fs[:, 20 * j:20 * j + 20], False, j == 2, ["blk", "fs"], "pr")
-    mm(T.pm[:, 0:2], T.blk[:], T.fs[:, 39:60:20], True, True, ["blk", "fs"], "pm")
+    mm(T.pm[:, 0:2], T.blk[:], T.fs[:, 39:60:20], True, False, ["blk", "fs"], "pm")
+    mm(T.pm[:, 0:1], T.nblk[:], T.fs[:, 59:60], False, True, ["nblk", "fs"], "pm")
     scan(T.mx[:], T.d0d[:], T.pr[:, 0:80], A.min, A.max, r=["d0d"], w=["mx"], b="pr", n=80)
     act(T.win2[:, 640:641], T.pm[:, 1:2], 1.0, float(LB), r=["cnt"], w=["cn0"], b="pm")
     act(T.win2[:, 641:642], T.pm[:, 1:2], -1.0, float(RB - LB), r=["cnt"], w=["cn1"], b="pm")
@@ -561,6 +558,10 @@ def rank_program(g, core, T, topo):
         moved = list(level)
         for i in rng.integers(0, n_ops, 6):
             moved[int(i)] += float(rng.normal(0, 1)) * (300 if turn % 2 else 2500)
+        if turn % 3 == 0:
+            a, shift = int(rng.integers(0, n_ops)), float(rng.normal(0, 500))
+            for i in range(a, min(n_ops, a + int(rng.integers(3, 30)))):
+                moved[i] += shift
         cand = place(moved)
         size = length(cand)
         if size <= best:

@@ -2,22 +2,23 @@ import numpy as np
 from concourse.bass import DstId, RemoteDMATransfer
 from concourse.mybir import AluOpType as A, ActivationFunctionType as F
 
-NS1, NS2 = 5, 10
+NS1, NS2 = 6, 8
 CUT1, CUT2 = (0, 6, 12, 16), (0, 6, 14, 20)
-LAT, PE = 150, 0.52
-TRY, ROUNDS = ((100, 1.0), (180, 1.2)), 1500
+LAT, PE = 180, 0.52
+TRY, ROUNDS = ((150, 1.0), (210, 1.2)), 1800
+FAR, FIRST = 1800, 1300
 B = 2.0 ** 40
 SB, LB, RB, ZC = 352, 648, 688, 720
 
 f32, bf, f16, i32, u16 = "float32", "bfloat16", "float16", "int32", "uint16"
 _S = {
     i32: "xi 16 vi 16 wi 16 li 4 rows 256 seg 640 kraw 128 pi 8 lo 16 xpi 16",
-    bf: "ktab 128 pa 128 grow 128 cv 132 blk 128 blkh 128 ident 128 ir0 128 ni 128 l1 128 r1 128 t1 128 t2 128 sn 128 "
+    bf: "ktab 128 pa 128 grow 128 cv 132 blk 128 blkh 128 ident 128 ir0 128 ni 128 l1 128 r1 128 t2 128 sn 128 "
         "sp 128 d0a 32 d0b 60 adj 320 adjl 128 sg 16 q2 32 tot 16 land0 8 cellb 16 rh 2112 hb 256 mask 320 kk 320 "
         "aa 320 fl 60 fs 60 nt2 128 nblk 128 fq 32",
     f16: "identh 128 lpay 128 l20 128 l21 128 loe 160 cc 320",
     u16: "jt16 16 cello 16 offe 8 uo16 20 xo16 20 off 40 dst 20 o16 16",
-    f32: "jraw 20 jidx 20 tv 24 col 40 e16 16 bb 8 tmp 48 mb16 256 mb8 192 jt 16 identf 128 inr1 128 sel0 128 sel1 128 "
+    f32: "jraw 20 jidx 20 tv 24 col 40 e16 16 bb 8 tmp 48 mb16 256 mb8 128 jt 16 identf 128 inr1 128 sel0 128 sel1 128 "
          "d0c 48 d0d 80 cr1 48 cr2 80 c64 4 al 16 qf 16 v64 16 nqc 16 xmb 16 y0 16 y1 20 thl 20 thr 20 thg 20 zz 20 "
          "tt 136 eg 256 se 256 ve0 16 stat 256 pay 320 a0 80 a1 80 b0 80 b1 80 b2 64 xo 4 sc 160 sx 320 mx 80 junk 48 "
          "win1 336 land1 72 landx 4 win2 728 xpb 16 uon 16 al2 16 al1 16 hc 16 c127 20 sin 128 ii 24 oo 64 res 256",
@@ -42,7 +43,7 @@ def rank_program(g, core, T, topo):
     sem = T.sem
     Q = {"v": g.vector, "s": g.scalar, "p": g.tensor, "g": g, "y": g.sync}
     own = {"v": "sv", "s": "ss", "p": "sp", "g": "sg"}
-    ops, wr, rd, bank, issue = [], {}, {}, {}, [1900]
+    ops, wr, rd, bank, issue = [], {}, {}, {}, [FIRST]
 
     def add(e, fn, hold, lat, r=(), w=(), b=None, kind="op"):
         dep = {}
@@ -101,7 +102,10 @@ def rank_program(g, core, T, topo):
         else:
             add("g", lambda: g.iota(out, pattern, base, mult, allow_small_or_imprecise_dtypes=True), t, t, (), w)
 
-    def dma(e, out, in_, r=(), w=(), lat=1900):
+    def select(out, in_, op, fill):
+        add("g", lambda: g.affine_select(T[out][:], T[in_][:], [[-1, 128]], op, fill, 0, 1), 480, 480, [in_], [out])
+
+    def dma(e, out, in_, r=(), w=(), lat=1600):
         add(e, lambda: Q[e].dma_start(out, in_), 60, lat, r, w, None, "dma")
 
     def send(items, s, r, w):
@@ -195,10 +199,10 @@ def rank_program(g, core, T, topo):
     ts(T.l21[:, 0::2], T.blk[:, 0::2], 0.0, A.mult, r=["blk"], w=["l21a"])
     ts(T.l21[:, 1::2], T.blk[:, 1::2], 1.0, A.mult, r=["blk"], w=["l21b"])
     cp(T.identh[:], T.ident[:], r=["ident"], w=["identh"])
-    ts(T.t1[:], MR, c(G16), A.subtract, 1.5, A.is_le, r=["cv0", k(G16)], w=["t1"])
-    ts(T.t2[:], MR, PCOL, A.is_lt, -1.0, A.mult, r=["cv0", "jraw"], w=["t2"])
-    tt(T.lpay[:], T.t1[:], T.blk[:], A.mult, r=["t1", "blk"], w=["lpay"], n=256)
-    tt(T.t2[:], T.t2[:], T.blk[:], A.mult, r=["blk"], w=["t2"], n=256)
+    ts(T.lpay[:], T.blk[:], 0.0, A.mult, r=["blk"], w=["lpay"])
+    cp(T.lpay[:, 0::16], T.blk[:, 0::16], r=["blk", "lpay"], w=["lpa"])
+    cp(T.lpay[:, 1::16], T.blk[:, 1::16], r=["blk", "lpay"], w=["lpb"])
+    select("nt2", "blk", A.is_gt, 0.0)
 
     act(T.cv[:, 128:129], c(RF), 0.0, -1000.0, r=[k(RF)], w=["cv1"])
     act(c(MKB), c(RF), -1.0, 192.0 - 255.5 / 512.0, r=[k(RF)], w=[k(MKB)])
@@ -208,16 +212,16 @@ def rank_program(g, core, T, topo):
     act(c(NR1), E1, -1.0, 1.0, r=["e16"], w=[k(NR1)])
     for n, src, f, r in (("blkh", "blk", 0.5, []), ("sel0", "blk", E0, ["e16"]), ("sel1", "blk", E1, ["e16"]),
                          ("ni", "ident", -1024.0, []), ("inr1", "ident", c(NR1), [k(NR1)]),
-                         ("ir0", "ident", E0, ["e16"]), ("identf", "ident", 1.0, []), ("nt2", "t2", -1.0, []),
+                         ("ir0", "ident", E0, ["e16"]), ("identf", "ident", 1.0, []), ("t2", "nt2", -1.0, []),
                          ("nblk", "blk", -1.0, [])):
         act(T[n][:], T[src][:], f, r=[src] + r, w=[n], n=128)
+    select("r1", "t2", A.not_equal, 1024.0)
     act(T.sn[:, 0:127], T.ident[:, 1:128], r=["ident"], w=["sn"], n=128)
     act(T.sp[:, 1:128], T.ident[:, 0:127], r=["ident"], w=["sp"], n=128)
     act(T.sn[:, 15::16], T.ident[:, 0::16], r=["ident"], w=["sn"])
     act(T.sp[:, 0::16], T.ident[:, 15::16], r=["ident"], w=["sp"])
     act(T.l1[:, 0::2], T.blk[:, 0::2], 128.0, r=["blk"], w=["l1a"])
     act(T.l1[:, 1::2], T.blk[:, 1::2], -128.0, r=["blk"], w=["l1b"])
-    tt(T.r1[:], T.t2[:], T.ni[:], A.subtract, r=["t2", "ni"], w=["r1"], n=256)
     for i, src, f in ((NB8, B8, -1.0), (C40, B8, -4032.0), (C41, B8, 4160.0), (N8B, B8, 8192.0), (B127, B16, 127.0)):
         act(c(i), src, f, r=["bb"], w=[k(i)])
     for i, f in ((P9, 8492.0), (M9, -212.0), (P8, 8192.0), (M8, -8192.0), (PB0, -64.0)):
@@ -244,7 +248,7 @@ def rank_program(g, core, T, topo):
         scan(T.tot[:], T.d0a[:, 0:16], T.q2[:, 0:16], A.min, A.add, r=["d0a", "q"], w=["tot"])
         send([(T.tot[:, 15:16], [(cores[d], T.land0[:, rank:rank + 1]) for d in range(N - 1, rank, -1)], eng)],
              "x1", ["tot"], ["sent1"])
-    arrive("land0", "x1", ne * rank, ["q", "sent1"], 2800 if rank < N - 1 else 4700)
+    arrive("land0", "x1", ne * rank, ["q", "sent1"], FAR if rank < N - 1 else FAR + FIRST)
 
     def field(ns, src, key):
         ts(T.hc[:], T.cellb[:], -1.0, A.mult, 0.5, A.add, r=["cellb"], w=["hc"])
@@ -252,8 +256,6 @@ def rank_program(g, core, T, topo):
         ts(T.cello[:], T.cellb[:], -128.0, A.add, 127.0, A.min, r=["cellb"], w=["cello"])
         vs, ss_ = list(range(16 - ns)), list(range(16 - ns, 16))
         order = []
-        if ns > 8:
-            order, ss_ = ss_[:ns - 2], ss_[ns - 2:]
         while vs or ss_:
             order += vs[:2] + ss_[:1]
             vs, ss_ = vs[2:], ss_[1:]
@@ -350,7 +352,7 @@ def rank_program(g, core, T, topo):
                 mm(PU[:, 0:n], T.l20[:], ev, True, False, ["l20a", "l20b", ck], ub, m1)
                 mm(PU[:, 0:n], T.l21[:], od, False, True, ["l21a", "l21b", ck], ub, m1)
                 if i == 2:
-                    mm(T.pp[:, 16 * a:16 * e], T.lpay[:], CC_, False, h == nch - 1, ["lpay", ck], "pp", m2)
+                    mm(T.pp[:, 16 * a:16 * e], T.lpay[:], CC_, False, h == nch - 1, ["lpa", "lpb", ck], "pp", m2)
                     scan(T.sc[:, 8 * a:8 * e], T.mb8[:, 0:n], PU[:, 0:n], A.mult, A.add, r=["mb8"],
                          w=["sc%d" % h], b=ub, n=n)
                 else:
@@ -388,10 +390,10 @@ def rank_program(g, core, T, topo):
     fx = ["fx%d" % i for i in range(len(fluxes))]
     if rank in (0, N - 1):
         send([(T.win1[:, 4:5], [(cores[(rank + 2) % N], T.landx[:, 0:1])], eng)], "x2", ["fx0"], ["sentx"])
-        arrive("landx", "x2", 0, ["sentx"], 2400)
+        arrive("landx", "x2", 0, ["sentx"], FAR - 300)
     send([(T.win1[:, 4:40], [(right, T.land1[:, 0:36])], eng[:half]),
           (T.win1[:, 296:332], [(left, T.land1[:, 36:72])], eng[half:])], "x2", ["win1", "sentx"] + fx, ["sent2"])
-    arrive("land1", "x2", ne if rank in (0, N - 1) else 2 * ne, ["sent2"], 2400)
+    arrive("land1", "x2", ne if rank in (0, N - 1) else 2 * ne, ["sent2"], FAR)
 
     ts(T.cellb[:], T.xpb[:], c(IB64), A.mult, 128.0 - 31.5 / 64, A.add, r=["xpb", k(IB64)], w=["cellb"])
     ts(T.xpi[:], T.xpb[:], IB8, A.mult, r=["xpb", "ib"], w=["xpi"])
@@ -442,7 +444,7 @@ def rank_program(g, core, T, topo):
     first()
     scan(T.sin[:], T.mb16[:, 0:128], T.pm[:, 0:128], A.mult, A.add, r=["mb16"], w=["sin"], b="pm", n=128)
     I2 = T.sin[:, 79:128:16]
-    act(I0, T.b1[:, 65:80:4], B16, r=["b1", "bb"], w=["i0"])
+    ts(I0, T.b1[:, 65:80:4], B16, A.mult, r=["b1", "bb"], w=["i0"])
     act(I4, I2, IB16, r=["sin", "ib"], w=["i4"])
     tt(I1, I0, T.sin[:, 15:64:16], A.add, r=["i0", "sin"], w=["i1"])
     ts(I3, I1, B16, A.max, c(B127), A.min, r=["i1", k(B127)], w=["i3"])
@@ -482,7 +484,7 @@ def rank_program(g, core, T, topo):
     send([(T.win2[:, 608:644], [(right, T.win2[:, LB:LB + 36])], eng[:half]),
           (T.win2[:, 316:352], [(left, T.win2[:, RB - 4:RB + 32])], eng[half:])], "x3", ["win2", "cn0", "cn1"],
          ["sent3"])
-    arrive("land2", "x3", ne, ["sent3"], 2800)
+    arrive("land2", "x3", ne, ["sent3"], FAR)
     ts(O0, T.jt[:], c(NS), A.is_ge, c(EC), A.mult, r=["jt", k(NS), k(EC)], w=["o0"])
     ts(O1, T.jt[:], float(SB), A.add, r=["jt"], w=["o1"])
     tt(O2, O0, O1, A.add, r=["o0", "o1"], w=["o2"])

import numpy as np
from concourse.bass import DstId, RemoteDMATransfer
from concourse.mybir import AluOpType as A, ActivationFunctionType as F

NS1, NS2 = 6, 8
CUT1, CUT2 = (0, 6, 12, 16), (0, 6, 14, 20)
LAT, PE = 180, 0.52
TRY, ROUNDS = ((150, 1.0), (210, 1.2)), 1800
FAR, FIRST = 1800, 1300
B = 2.0 ** 40
SB, LB, RB, ZC = 352, 648, 688, 720

f32, bf, f16, i32, u16 = "float32", "bfloat16", "float16", "int32", "uint16"
_S = {
    i32: "xi 16 vi 16 wi 16 li 4 rows 256 seg 640 kraw 128 pi 8 lo 16 xpi 16",
    bf: "ktab 128 pa 128 grow 128 cv 132 blk 128 blkh 128 ident 128 ir0 128 ni 128 l1 128 r1 128 t2 128 sn 128 "
        "sp 128 d0a 32 d0b 60 adj 320 adjl 128 sg 16 q2 32 tot 16 land0 8 cellb 16 rh 2112 hb 256 mask 320 kk 320 "
        "aa 320 fl 60 fs 60 nt2 128 nblk 128 fq 32",
    f16: "identh 128 lpay 128 l20 128 l21 128 loe 160 cc 320",
    u16: "jt16 16 cello 16 offe 8 uo16 20 xo16 20 off 40 dst 20 o16 16",
    f32: "jraw 20 jidx 20 tv 24 col 40 e16 16 bb 8 tmp 48 mb16 256 mb8 128 jt 16 identf 128 inr1 128 sel0 128 sel1 128 "
         "d0c 48 d0d 80 cr1 48 cr2 80 c64 4 al 16 qf 16 v64 16 nqc 16 xmb 16 y0 16 y1 20 thl 20 thr 20 thg 20 zz 20 "
         "tt 136 eg 256 se 256 ve0 16 stat 256 pay 320 a0 80 a1 80 b0 80 b1 80 b2 64 xo 4 sc 160 sx 320 mx 80 junk 48 "
         "win1 336 land1 72 landx 4 win2 728 xpb 16 uon 16 al2 16 al1 16 hc 16 c127 20 sin 128 ii 24 oo 64 res 256",
}
SCRATCH = {n: ("sbuf", [128, int(w)], d) for d, t in _S.items() for n, w in zip(t.split()[0::2], t.split()[1::2])}
for _k in ("py0", "py1", "pu0", "pu1", "pp", "pt", "pr", "pm"):
    SCRATCH[_k] = ("psum", [128, 512], f32)

SEMAPHORES = ["sv", "ss", "sp", "sg", "ls", "x1", "x2", "x3"] + ["d%d" % i for i in range(12)]

(RF, G16, NF, SGN, BQ, BQ1, PAYB, MKB, NR1, P8, M8, NB8, C40, C41, N8B, B127, R8, IB64, R16, PC, CC, EC, P9, M9, PB0,
 NS) = range(26)


def rank_program(g, core, T, topo):
    rank = T.rank_of(core)
    if rank is None:
        return
    cores = list(T.cores)
    N = len(cores)
    left, right = cores[(rank - 1) % N], cores[(rank + 1) % N]
    sem = T.sem
    Q = {"v": g.vector, "s": g.scalar, "p": g.tensor, "g": g, "y": g.sync}
    own = {"v": "sv", "s": "ss", "p": "sp", "g": "sg"}
    ops, wr, rd, bank, issue = [], {}, {}, {}, [FIRST]

    def add(e, fn, hold, lat, r=(), w=(), b=None, kind="op"):
        dep = {}
        for n in r:
            if n in wr:
                dep[wr[n]] = True
        for n in w:
            for d in ([wr[n]] if n in wr else []) + rd.get(n, []):
                dep[d] = True
        if b in bank:
            d = bank[b]
            dep[d] = dep.get(d, False) or ops[d]["e"] != e
        i = len(ops)
        ops.append({"e": e, "fn": fn, "hold": hold, "lat": lat, "dep": dep, "kind": kind})
        for n in r:
            rd.setdefault(n, []).append(i)
        for n in w:
            wr[n] = i
            rd[n] = []
        if b is not None:
            bank[b] = i

    def vop(fn, n, r, w, b):
        t = max(64, n) * 1.04
        add("v", fn, t, t, r, w, b)

    def ts(out, in0, s1, o0, s2=None, o1=None, r=(), w=(), b=None, n=0):
        if o1 is None:
            vop(lambda: g.vector.tensor_scalar(out, in0, s1, None, o0), n, r, w, b)
        else:
            vop(lambda: g.vector.tensor_scalar(out, in0, s1, s2, o0, o1), n, r, w, b)

    def tt(out, in0, in1, o, r=(), w=(), b=None, n=0):
        vop(lambda: g.vector.tensor_tensor(out, in0, in1, o), n, r, w, b)

    def cp(out, in_, r=(), w=(), b=None, n=0):
        vop(lambda: g.vector.tensor_copy(out, in_), n, r, w, b)

    def scan(out, d0, d1, o0, o1, r=(), w=(), b=None, n=0):
        vop(lambda: g.vector.tensor_tensor_scan(out, d0, d1, 0.0, o0, o1), n, r, w, b)

    def act(out, in_, scale=1.0, bias=0.0, func=F.Identity, acc=None, r=(), w=(), b=None, n=0):
        t = max(64, n) * 1.04 + 15
        add("s", lambda: g.scalar.activation(out, in_, func, bias=bias, scale=scale, accum_out=acc), t, t, r, w, b)

    def mm(out, lhsT, rhs, start, stop, r, b, n=64):
        add("p", lambda: g.tensor.matmul(out, lhsT, rhs, start, stop), n * PE, n * PE, r, (), b)

    def iota(out, pattern, base, mult, w, integer=False):
        n = 1
        for _, m in pattern:
            n *= m
        t = 165 + 2.1 * n
        if integer:
            add("g", lambda: g.iota(out, pattern, base, mult), t, t, (), w)
        else:
            add("g", lambda: g.iota(out, pattern, base, mult, allow_small_or_imprecise_dtypes=True), t, t, (), w)

    def select(out, in_, op, fill):
        add("g", lambda: g.affine_select(T[out][:], T[in_][:], [[-1, 128]], op, fill, 0, 1), 480, 480, [in_], [out])

    def dma(e, out, in_, r=(), w=(), lat=1600):
        add(e, lambda: Q[e].dma_start(out, in_), 60, lat, r, w, None, "dma")

    def send(items, s, r, w):
        trs = []
        for src, dd, engs in items:
            ids = [DstId(rid=topo.addr(d)[0], pnc=topo.addr(d)[1]) for d, _ in dd]
            trs.append(RemoteDMATransfer(dst_ids=ids, dma_engine_mask=sum(1 << e for e in engs), remote_sem=sem[s],
                                         srcs=[src], dsts=[o for _, o in dd]))
        add("g", (trs, sum(len(x[2]) for x in items)), issue[0], issue[0], r, w, None, "send")
        issue[0] = 400

    def arrive(key, s, n, after, lat):
        add(None, (s, n), 0, lat, after, [key], None, "arrive")

    def gat(n):
        return 60 + 1.56 * n

    def c(i):
        return T.col[:, i:i + 1]

    def k(i):
        return "c%d" % i

    eng = topo.engines(core, right)
    ne = len(eng)
    half = ne // 2
    B8, B16, IB8, IB16 = T.bb[:, 2:3], T.bb[:, 3:4], T.bb[:, 4:5], T.bb[:, 5:6]
    I0, I1, I3, I4 = T.ii[:, 0:4], T.ii[:, 4:8], T.ii[:, 12:16], T.ii[:, 16:20]
    O0, O1, O2, O3 = T.oo[:, 0:16], T.oo[:, 16:32], T.oo[:, 32:48], T.oo[:, 48:64]
    MR, PCOL, ANY = T.cv[:, 0:128], T.jraw[:, 0:1], T.cv[:, 0:32]
    E0, E1 = T.e16[:, 0:1], T.e16[:, 1:2]

    dma("y", T.wi[:], T.w[:], w=["wi"])
    dma("s", T.li[:, 0:1], T.live[:], w=["li"])
    dma("y", T.xi[:], T.x[:], w=["xi"])
    dma("s", T.seg[:, 64:576], T.med[:], w=["segm"], lat=3000)
    vop(lambda: g.vector.memset(T.rows[:], 0), 256, (), ["rows"], None)
    dma("y", T.rows[0::16, :], T.x[:], r=["rows"], w=["rowx"])
    dma("y", T.rows[2::16, :], T.w[:], r=["rows"], w=["roww"])
    dma("y", T.vi[:], T.v[:], w=["vi"])
    dma("y", T.kraw[:], T.kick[:], w=["kraw"], lat=2200)

    iota(T.pi[:, 0:1], [[0, 1]], 0, 1, ["pi"], True)
    iota(T.jraw[:], [[16, 20]], 128, 1, ["jraw"])
    for out, pat, base, w in (
            (T.tv[:], [[1, 24]], -3, ["tv"]), (T.grow[:], [[16, 8], [0, 16]], 128, ["grow"]),
            (T.d0a[:], [[0, 2], [64, 16]], 0, ["d0a"]), (MR, [[1, 128]], 128, ["cv0"]),
            (T.b1[:], [[0, 20], [1000, 4]], -1873, ["b1"]), (T.b0[:], [[0, 20], [-10000, 4]], 20000, ["b0"]),
            (T.a1[:], [[0, 20], [1000, 4]], -1873, ["a1", "ve", "vel", "ver"]), (T.a1[:, 1:64:4], [[0, 16]], 1, ["a1"]),
            (T.a1[:, 65:80:4], [[0, 4]], -10000, ["a1"]), (T.a0[:], [[0, 80]], -30000, ["a0"]),
            (T.win1[:], [[0, 336]], 0, ["win1", "fx"]), (T.d0c[:], [[0, 16], [10000, 3]], 0, ["d0c"]),
            (T.cr1[:, 1::3], [[0, 16]], -1025, ["cr1b"]), (T.cr1[:, 2::3], [[0, 16]], 288 - 1025, ["cr1c"]),
            (T.c64[:], [[0, 4]], 64, ["c64"]), (T.adjl[:, 0:64], [[0, 64]], 0, ["adjk"]),
            (T.adjl[:, 64:128], [[8704, 2], [0, 32]], -8192, ["adjl"]),
            (T.c127[:, 16:20], [[1, 2], [0, 2]], -1 if rank == N - 1 else 0, ["c127b"]),
            (T.adj[:, 0:256], [[0, 256]], 0, ["adja"]), (T.adj[:, 256:320], [[16384, 2], [0, 32]], -8192, ["adjb"]),
            (T.win2[:, 0:320], [[0, 320]], 0, ["win2"]), (T.win2[:, 320:LB], [[0, LB - 320]], 0, ["win2b", "cnt"]),
            (T.win2[:, ZC:728], [[0, 8]], 0, ["zc"]), (T.d0b[:], [[0, 3], [64, 20]], 0, ["d0b"]),
            (T.d0d[:], [[0, 20], [10000, 4]], 0, ["d0d"]), (T.cr2[:, 1::4], [[0, 20]], 320 - 1025, ["cr2b"]),
            (T.cr2[:, 2::4], [[0, 20]], SB - 1025, ["cr2c"]), (T.cr2[:, 3::4], [[0, 20]], 608 - 1025, ["cr2d"])):
        iota(out, pat, base, 0, w)

    TR = ["tv", k(RF)]
    ts(T.pi[:, 1:2], T.pi[:, 0:1], 15, A.bitwise_and, r=["pi"], w=["ri"])
    ts(T.pi[:, 2:3], T.pi[:, 0:1], 1, A.bitwise_and, r=["pi"], w=["par"])
    cp(c(RF), T.pi[:, 1:2], r=["ri"], w=[k(RF)])
    ts(c(SGN), T.pi[:, 2:3], -256.0, A.mult, 128.0, A.add, r=["par"], w=[k(SGN)])
    ts(c(G16), PCOL, c(RF), A.subtract, r=["jraw", k(RF)], w=[k(G16)])
    ts(T.tmp[:, 0:16], T.tv[:, 2:18], c(RF), A.is_ge, B, A.mult, r=TR, w=["tm0"])
    ts(T.tmp[:, 16:32], T.tv[:, 1:17], c(RF), A.is_lt, 1.0 / B, A.max, r=TR, w=["tm1"])
    ts(T.tmp[:, 32:40], T.tv[:, 2:18:2], c(RF), A.is_ge, B, A.mult, r=TR, w=["tm2"])
    ts(T.tmp[:, 40:48], T.tv[:, 0:16:2], c(RF), A.is_lt, 1.0 / B, A.max, r=TR, w=["tm3"])
    tt(T.mb16[:, 0:16], T.tmp[:, 0:16], T.tmp[:, 16:32], A.mult, r=["tm0", "tm1"], w=["mb16"])
    tt(T.mb8[:, 0:8], T.tmp[:, 32:40], T.tmp[:, 40:48], A.mult, r=["tm2", "tm3"], w=["mb8"])
    ts(T.e16[:], T.tv[:, 3:19], c(RF), A.is_equal, r=TR, w=["e16"])
    ts(T.bb[:, 0:2], T.tv[:, 17:19], c(RF), A.is_gt, B, A.mult, r=TR, w=["bb0"])
    ts(T.bb[:, 4:6], T.tv[:, 17:19], c(RF), A.is_le, 1.0 / B, A.max, r=TR, w=["ib"])
    ts(T.jidx[:], T.jraw[:], c(G16), A.subtract, r=["jraw", k(G16)], w=["jidx"])
    ts(T.bb[:, 2:4], T.bb[:, 0:2], 1.0, A.max, r=["bb0"], w=["bb"])
    ts(c(R16), c(RF), 16.0, A.mult, r=[k(RF)], w=[k(R16)])
    ts(c(R8), c(RF), 7.5, A.is_gt, r=[k(RF)], w=[k(R8)])
    ts(T.blk[:], T.grow[:], c(G16), A.is_equal, r=["grow", k(G16)], w=["blk"])
    ts(T.jt[:], T.tv[:, 3:19], c(R16), A.add, r=["tv", k(R16)], w=["jt"])
    ts(T.jt16[:], T.tv[:, 3:19], c(R16), A.add, r=["tv", k(R16)], w=["jt16"])
    ts(T.offe[:], T.tv[:, 3:19:2], c(R8), A.add, r=["tv", k(R8)], w=["offe"])
    ts(T.ident[:], MR, PCOL, A.is_equal, r=["cv0", "jraw"], w=["ident"])
    ts(c(BQ), c(SGN), c(RF), A.mult, r=[k(SGN), k(RF)], w=[k(BQ)])
    ts(c(BQ1), c(SGN), c(RF), A.mult, 128.0, A.add, r=[k(SGN), k(RF)], w=[k(BQ1)])
    ts(T.l20[:, 0::2], T.blk[:, 0::2], 1.0, A.mult, r=["blk"], w=["l20a"])
    ts(T.l20[:, 1::2], T.blk[:, 1::2], 0.0, A.mult, r=["blk"], w=["l20b"])
    ts(T.l21[:, 0::2], T.blk[:, 0::2], 0.0, A.mult, r=["blk"], w=["l21a"])
    ts(T.l21[:, 1::2], T.blk[:, 1::2], 1.0, A.mult, r=["blk"], w=["l21b"])
    cp(T.identh[:], T.ident[:], r=["ident"], w=["identh"])
    ts(T.lpay[:], T.blk[:], 0.0, A.mult, r=["blk"], w=["lpay"])
    cp(T.lpay[:, 0::16], T.blk[:, 0::16], r=["blk", "lpay"], w=["lpa"])
    cp(T.lpay[:, 1::16], T.blk[:, 1::16], r=["blk", "lpay"], w=["lpb"])
    select("nt2", "blk", A.is_gt, 0.0)

    act(T.cv[:, 128:129], c(RF), 0.0, -1000.0, r=[k(RF)], w=["cv1"])
    act(c(MKB), c(RF), -1.0, 192.0 - 255.5 / 512.0, r=[k(RF)], w=[k(MKB)])
    for n0 in (16, 32, 64, 128):
        act(T.mb16[:, n0:2 * n0], T.mb16[:, 0:n0], w=["mb16"], n=n0)
        act(T.mb8[:, n0 // 2:n0], T.mb8[:, 0:n0 // 2], w=["mb8"])
    act(c(NR1), E1, -1.0, 1.0, r=["e16"], w=[k(NR1)])
    for n, src, f, r in (("blkh", "blk", 0.5, []), ("sel0", "blk", E0, ["e16"]), ("sel1", "blk", E1, ["e16"]),
                         ("ni", "ident", -1024.0, []), ("inr1", "ident", c(NR1), [k(NR1)]),
                         ("ir0", "ident", E0, ["e16"]), ("identf", "ident", 1.0, []), ("t2", "nt2", -1.0, []),
                         ("nblk", "blk", -1.0, [])):
        act(T[n][:], T[src][:], f, r=[src] + r, w=[n], n=128)
    select("r1", "t2", A.not_equal, 1024.0)
    act(T.sn[:, 0:127], T.ident[:, 1:128], r=["ident"], w=["sn"], n=128)
    act(T.sp[:, 1:128], T.ident[:, 0:127], r=["ident"], w=["sp"], n=128)
    act(T.sn[:, 15::16], T.ident[:, 0::16], r=["ident"], w=["sn"])
    act(T.sp[:, 0::16], T.ident[:, 15::16], r=["ident"], w=["sp"])
    act(T.l1[:, 0::2], T.blk[:, 0::2], 128.0, r=["blk"], w=["l1a"])
    act(T.l1[:, 1::2], T.blk[:, 1::2], -128.0, r=["blk"], w=["l1b"])
    for i, src, f in ((NB8, B8, -1.0), (C40, B8, -4032.0), (C41, B8, 4160.0), (N8B, B8, 8192.0), (B127, B16, 127.0)):
        act(c(i), src, f, r=["bb"], w=[k(i)])
    for i, f in ((P9, 8492.0), (M9, -212.0), (P8, 8192.0), (M8, -8192.0), (PB0, -64.0)):
        act(c(i), E0, f, r=["e16"], w=[k(i)])
    act(c(PAYB), E1, -64.0, c(PB0), r=["e16", k(PB0)], w=[k(PAYB)])
    act(c(IB64), IB8, 1.0 / 64, r=["ib"], w=[k(IB64)])
    act(T.cr1[:, 0::3], T.jidx[:, 0:16], bias=32.0, r=["jidx"], w=["cr1a"])
    act(T.cr2[:, 0::4], T.jidx[:], r=["jidx"], w=["cr2a"])
    act(T.mask[:, 256:288], ANY, 0.0, E0, r=["cv0", "e16"], w=["maskl"])
    act(T.mask[:, 288:320], ANY, 0.0, T.e16[:, 15:16], r=["cv0", "e16"], w=["maskr"])
    act(T.win1[:, 8:40], ANY, 0.0, c(P9), r=["cv0", k(P9)], w=["win1"])
    act(T.win1[:, 296:328], ANY, 0.0, c(M9), r=["cv0", k(M9)], w=["win1"])
    act(T.win2[:, 320:352], ANY, 0.0, c(M8), r=["cv0", k(M8)], w=["win2b"])
    act(T.win2[:, 608:640], ANY, 0.0, c(P8), r=["cv0", k(P8)], w=["win2b"])

    cp(c(NF), T.li[:, 0:1], r=["li"], w=[k(NF)])
    ts(T.sg[:], T.wi[:], -1.0, A.max, 1.0, A.min, r=["wi"], w=["sg"])
    ts(T.al[:], T.jidx[:, 0:16], c(NF), A.is_lt, r=["jidx", k(NF)], w=["al"])
    ts(T.cellb[:], T.xi[:], 1.0 / 64, A.mult, 128.0 - 31.5 / 64, A.add, r=["xi"], w=["cellb"])
    tt(T.q2[:, 0:16], T.sg[:], T.al[:], A.mult, r=["sg", "al"], w=["q"])
    tt(T.qf[:], T.sg[:], T.al[:], A.mult, r=["sg", "al"], w=["qf"])
    act(T.q2[:, 16:32], T.q2[:, 0:16], r=["q"], w=["qb"])
    if rank < N - 1:
        scan(T.tot[:], T.d0a[:, 0:16], T.q2[:, 0:16], A.min, A.add, r=["d0a", "q"], w=["tot"])
        send([(T.tot[:, 15:16], [(cores[d], T.land0[:, rank:rank + 1]) for d in range(N - 1, rank, -1)], eng)],
             "x1", ["tot"], ["sent1"])
    arrive("land0", "x1", ne * rank, ["q", "sent1"], FAR if rank < N - 1 else FAR + FIRST)

    def field(ns, src, key):
        ts(T.hc[:], T.cellb[:], -1.0, A.mult, 0.5, A.add, r=["cellb"], w=["hc"])
        tt(T.nqc[:], T.qf[:], T.hc[:], A.mult, r=["qf", "hc"], w=["nqc"])
        ts(T.cello[:], T.cellb[:], -128.0, A.add, 127.0, A.min, r=["cellb"], w=["cello"])
        vs, ss_ = list(range(16 - ns)), list(range(16 - ns, 16))
        order = []
        while vs or ss_:
            order += vs[:2] + ss_[:1]
            vs, ss_ = vs[2:], ss_[1:]
        for i, j in enumerate(order):
            h = j >= 16 - ns
            o = T.rh[:, 132 * j:132 * j + 129]
            if h:
                act(o, T.cv[:, 0:129], T.qf[:, j:j + 1], T.nqc[:, j:j + 1], F.Sign, r=["cv0", "cv1", "qf", "nqc"],
                    w=["rh%d" % j], n=129)
            else:
                ts(o, T.cv[:, 0:129], T.cellb[:, j:j + 1], A.is_ge, T.q2[:, j:j + 1], A.mult,
                   r=["cv0", "cv1", "cellb", "q"], w=["rh%d" % j])
            mm(T.pt[:, 0:129], T.blkh[:] if h else T.blk[:], o, i == 0, i == 15, ["rh%d" % j, "blkh", "blk"], "pt", 129)
        act(T.tt[:, 0:129], T.pt[:, 0:129], w=["tt"], b="pt", n=129)
        act(T.eg[:], T.tt[:, 0:128].indirect(T.cello[:]), r=["tt", "cello"], w=["eg"], n=gat(256))
        scan(T.se[:], T.mb16[:], T.eg[:], A.mult, A.add, r=["mb16", "eg"], w=["se"], n=256)
        mm(T.pm[:, 0:256], T.sel0[:], src, True, True, [key, "sel0"], "pm", 1024)
        act(T.hb[:], T.pm[:, 0:256], 1.0 / 512, c(MKB), r=[k(MKB)], w=["hb"], b="pm", n=256)
        ts(T.mask[:, 0:256], T.hb[:], 192.0, A.is_equal, r=["hb"], w=["mask"], n=128)

    def places(xint, key):
        ts(T.lo[:], xint, 511, A.bitwise_and, r=[key], w=["lo"])
        cp(T.loe[:, 0:128], T.lo[:].indirect(T.offe[:]), r=["lo", "offe"], w=["loe"], n=gat(128))
        cp(T.b0[:, 3:64:4], T.lo[:], r=["lo"], w=["b0"])
        ts(T.y0[:], xint, -4096.0, A.add, r=[key], w=["y0"])

    def limits(a, e, r, w):
        act(T.thl[:, a:e], T.y1[:, a:e], c(NB8), c(C40), r=r + [k(NB8), k(C40)], w=["thl" + w])
        act(T.thr[:, a:e], T.y1[:, a:e], c(NB8), c(C41), r=r + [k(NB8), k(C41)], w=["thr" + w])

    def first():
        scan(T.b2[:], T.b0[:, 0:64], T.b1[:, 0:64], A.add, A.min, r=["b0", "b1"], w=["b2"])
        cp(T.uo16[:, 0:16], T.b2[:, 2::4], r=["b2"], w=["uo16"])
        cp(T.xo16[:, 0:16], T.b2[:, 3::4], r=["b2"], w=["xo16"])

    cp(T.stat[:], T.rows[:].indirect(T.jt16[:]), r=["rows", "rowx", "roww", "jt16"], w=["stat"], n=gat(256))
    field(NS1, T.stat[:], "stat")
    cp(T.pa[:, 0:64], T.seg[:, 64:128], r=["segm"], w=["pa0"])
    cp(T.pa[:, 64:128], T.seg[:, 512:576], r=["segm"], w=["pa1"])
    mm(T.pu0[:, 0:64], T.sn[:], T.pa[:, 0:64], True, True, ["sn", "pa0"], "pu0")
    mm(T.pu0[:, 64:128], T.sp[:], T.pa[:, 64:128], True, True, ["sp", "pa1"], "pu0")
    cp(T.seg[:, 576:640], T.pu0[:, 0:64], w=["segr"], b="pu0")
    cp(T.seg[:, 0:64], T.pu0[:, 64:128], w=["segl"], b="pu0")
    ts(T.ktab[:], T.kraw[:], 64.0, A.add, r=["kraw"], w=["ktab"], n=128)
    ts(T.v64[:], T.vi[:], 64.0, A.add, r=["vi"], w=["v64"])
    places(T.xi[:], "xi")
    ts(T.ve0[:], T.se[:, 15::16], IB16, A.mult, T.tt[:, 128:129], A.subtract, r=["se", "ib", "tt"], w=["ve0"])
    tt(T.a1[:, 0:64:4], T.ve0[:], T.v64[:], A.add, r=["ve0", "v64"], w=["ve"])
    mm(T.pp[:, 0:256], T.inr1[:], T.stat[:], True, False, ["inr1", "stat"], "pp", 1024)
    tt(T.y1[:, 0:16], T.y0[:], T.al[:], A.mult, r=["y0", "al"], w=["y1"])
    limits(0, 16, ["y1"], "")
    ts(T.xmb[:], T.xi[:], -64.0, A.add, B8, A.mult, r=["xi", "bb"], w=["xmb"])

    if rank > 0:
        for d in range(rank):
            mm(T.pr[:, 0:1], T.blk[:], T.land0[:, d:d + 1], d == 0, d == rank - 1, ["blk", "land0"], "pr")
        ts(T.b1[:, 1:64:4], T.a1[:, 0:64:4], T.pr[:, 0:1], A.add, 1.0, A.max, r=["ve"], w=["b1"], b="pr")
        act(c(PC), T.pr[:, 0:1], w=[k(PC)], b="pr")
    else:
        ts(T.b1[:, 1:64:4], T.a1[:, 0:64:4], 1.0, A.max, r=["ve", "land0"], w=["b1"])
    first()
    mm(T.pr[:, 0:48], T.identf[:], T.cr1[:], True, False, ["identf", "cr1a", "cr1b", "cr1c"], "pr", 256)

    def scatterings(cut):
        nch = len(cut) - 1
        for i in range(3):
            for h in range(nch):
                a, e = cut[h], cut[h + 1]
                n = 8 * (e - a)
                m1, m2 = max(64, n), max(64, 2 * n)
                inc = e > 16
                yb, ub = ("py0", "py1", "pt")[h], ("pu0", "pu1", "pm")[h]
                PY, PU = T[yb], T[ub]
                kk, aa, ck, ok = "kk%d" % h, "aa%d" % h, "cc%d" % h, "off%d" % h
                K, AA, CC_ = T.kk[:, 16 * a:16 * e], T.aa[:, 16 * a:16 * e], T.cc[:, 16 * a:16 * e]
                ev, od = T.cc[:, 16 * a:16 * e:2], T.cc[:, 16 * a + 1:16 * e:2]
                if i == 0:
                    ou, ox = T.uo16[:, a:e], T.xo16[:, a:e]
                    ru, rx = ["uo16"] + ["uoi"] * inc, ["xo16"] + ["xoi"] * inc
                else:
                    ou, ox, ru, rx = T.off[:, 2 * a:a + e], T.off[:, a + e:2 * e], [ok], [ok]
                act(K, T.ktab[:].indirect(ou), r=["ktab"] + ru, w=[kk], n=gat(2 * n))
                tt(AA, T.seg[:].indirect(ox), T.mask[:, 16 * a:16 * e], A.mult,
                   r=["segm", "segl", "segr", "mask", "maskl", "maskr"] + rx, w=[aa], n=gat(2 * n))
                mm(PY[:, 0:2 * n], T.ident[:], K, True, False, ["ident", kk], yb, m2)
                mm(PY[:, 0:2 * n], T.l1[:], AA, False, True, ["l1a", "l1b", aa], yb, m2)
                if i < 2:
                    mm(PU[:, n:2 * n], T.identh[:], T.loe[:, 8 * a:8 * e], True, False,
                       ["identh", "loe"] + ["loi"] * inc, ub, m1)
                ts(CC_, PY[:, 0:2 * n], c(BQ), A.max, c(BQ1), A.min, r=[k(BQ), k(BQ1)], w=[ck], b=yb, n=2 * n)
                if i < 2:
                    mm(PU[:, n:2 * n], T.l20[:], ev, False, False, ["l20a", "l20b", ck], ub, m1)
                    mm(PU[:, n:2 * n], T.l21[:], od, False, True, ["l21a", "l21b", ck], ub, m1)
                mm(PU[:, 0:n], T.l20[:], ev, True, False, ["l20a", "l20b", ck], ub, m1)
                mm(PU[:, 0:n], T.l21[:], od, False, True, ["l21a", "l21b", ck], ub, m1)
                if i == 2:
                    mm(T.pp[:, 16 * a:16 * e], T.lpay[:], CC_, False, h == nch - 1, ["lpa", "lpb", ck], "pp", m2)
                    scan(T.sc[:, 8 * a:8 * e], T.mb8[:, 0:n], PU[:, 0:n], A.mult, A.add, r=["mb8"],
                         w=["sc%d" % h], b=ub, n=n)
                else:
                    scan(T.sx[:, 16 * a:16 * e], T.mb8[:, 0:2 * n], PU[:, 0:2 * n], A.mult, A.add, r=["mb8"],
                         w=["sx%d" % h], b=ub, n=2 * n)
                    ts(T.off[:, 2 * a:2 * e], T.sx[:, 16 * a + 7:16 * e:8], IB8, A.mult, r=["sx%d" % h, "ib"], w=[ok])
        return ["sc%d" % h for h in range(nch)]

    SC = scatterings(CUT1)

    U = T.sc[:, 7:128:8]
    act(T.pay[:, 0:256], T.pp[:, 0:256], 1.0, c(PAYB), r=[k(PAYB)], w=["pay"], b="pp", n=256)
    tt(T.fl[:, 0:16], U, T.thr[:, 0:16], A.is_ge, r=SC + ["thr"], w=["fr"])
    tt(T.fl[:, 16:32], U, T.thl[:, 0:16], A.is_lt, r=SC + ["thl"], w=["fl"])
    tt(T.xpb[:], U, T.xmb[:], A.add, r=SC + ["xmb"], w=["xpb"])
    scan(T.fs[:, 0:32], T.d0a[:], T.fl[:, 0:32], A.min, A.add, r=["d0a", "fr", "fl"], w=["fs"])
    mm(T.pr[:, 1:48:3], T.r1[:], T.fl[:, 0:16], False, False, ["r1", "fr"], "pr")
    mm(T.pr[:, 0:48:3], T.ni[:], T.fl[:, 0:16], False, False, ["ni", "fr"], "pr")
    mm(T.pr[:, 2:48:3], T.r1[:], T.fl[:, 16:32], False, False, ["r1", "fl"], "pr")
    mm(T.pr[:, 1:48:3], T.blk[:], T.fs[:, 0:16], False, False, ["blk", "fs"], "pr")
    mm(T.pr[:, 2:48:3], T.blk[:], T.fs[:, 16:32], False, True, ["blk", "fs"], "pr")
    scan(T.mx[:, 0:48], T.d0c[:], T.pr[:, 0:48], A.min, A.max, r=["d0c"], w=["mx"], b="pr")
    cp(T.dst[:, 0:16], T.mx[:, 2:48:3], r=["mx"], w=["dst"])
    cp(T.win1[:, 8:328].indirect(T.dst[:, 0:16]), T.pay[:, 0:256], r=["pay", "dst"], w=["win1"], n=60 + 3.8 * 256)
    tt(T.fq[:], T.fl[:, 0:32], T.q2[:], A.mult, r=["fr", "fl", "q", "qb"], w=["fq"])
    mm(T.pm[:, 0:32], T.blk[:], T.fq[:], True, True, ["blk", "fq"], "pm")
    fluxes = [(1, 328)]
    if rank == 0:
        fluxes = [(1, 4), (1, 328)]
    if rank == N - 1:
        fluxes = [(0, 4), (1, 328), (0, 329)]
    for i, (h, cidx) in enumerate(fluxes):
        act(T.junk[:, 16 * i:16 * i + 16], T.pm[:, 16 * h:16 * h + 16], acc=T.win1[:, cidx:cidx + 1], r=["fx"],
            w=["fx%d" % i], b="pm")
    fx = ["fx%d" % i for i in range(len(fluxes))]
    if rank in (0, N - 1):
        send([(T.win1[:, 4:5], [(cores[(rank + 2) % N], T.landx[:, 0:1])], eng)], "x2", ["fx0"], ["sentx"])
        arrive("landx", "x2", 0, ["sentx"], FAR - 300)
    send([(T.win1[:, 4:40], [(right, T.land1[:, 0:36])], eng[:half]),
          (T.win1[:, 296:332], [(left, T.land1[:, 36:72])], eng[half:])], "x2", ["win1", "sentx"] + fx, ["sent2"])
    arrive("land1", "x2", ne if rank in (0, N - 1) else 2 * ne, ["sent2"], FAR)

    ts(T.cellb[:], T.xpb[:], c(IB64), A.mult, 128.0 - 31.5 / 64, A.add, r=["xpb", k(IB64)], w=["cellb"])
    ts(T.xpi[:], T.xpb[:], IB8, A.mult, r=["xpb", "ib"], w=["xpi"])
    field(NS2, T.pay[:, 0:256], "pay")
    places(T.xpi[:], "xpi")
    ts(T.uon[:], U, IB8, A.mult, r=SC + ["ib"], w=["uon"])
    if rank == N - 1:
        ts(T.c127[:, 0:16], T.cellb[:], 255.0, A.is_equal, -1.0, A.add, r=["cellb"], w=["c127a"])
    else:
        ts(T.c127[:, 0:16], T.cellb[:], 255.0, A.is_equal, r=["cellb"], w=["c127a"])
    tt(T.al1[:], T.al[:], T.fl[:, 0:16], A.subtract, r=["al", "fr"], w=["al1"])
    tt(T.al2[:], T.al1[:], T.fl[:, 16:32], A.subtract, r=["al1", "fl"], w=["al2"])
    ts(T.zz[:, 0:16], T.al2[:], 0.5, A.is_lt, c(N8B), A.mult, r=["al2", k(N8B)], w=["zz"])
    tt(T.y1[:, 0:16], T.y0[:], T.al2[:], A.mult, r=["y0", "al2"], w=["y1"])
    limits(0, 16, ["y1"], "")
    tt(T.thg[:, 0:16], T.thl[:, 0:16], T.zz[:, 0:16], A.add, r=["thl", "zz"], w=["thg"])
    mm(T.pp[:, 0:320], T.ir0[:], T.adj[:], True, False, ["ir0", "adja", "adjb"], "pp", 320)
    mm(T.pp[:, 0:256], T.inr1[:], T.pay[:, 0:256], False, False, ["inr1", "pay"], "pp", 1024)
    mm(T.pr[:, 0:80], T.identf[:], T.cr2[:], True, False, ["identf", "cr2a", "cr2b", "cr2c", "cr2d"], "pr", 320)
    TX = T.tt[:, 128:129]
    if rank == 0:
        ts(c(CC), TX, -1.0, A.mult, T.win1[:, 328:329], A.subtract, r=["tt"] + fx, w=[k(CC)])
    elif rank == N - 1:
        ts(c(CC), c(PC), TX, A.subtract, T.win1[:, 329:330], A.add, r=["tt", k(PC)] + fx, w=[k(CC)])
    else:
        ts(c(CC), c(PC), TX, A.subtract, r=["tt", k(PC)], w=[k(CC)])
    ts(T.a1[:, 64:72:4], T.c64[:, 0:2], T.tt[:, 0:1], A.add, c(CC), A.add, r=["c64", "tt", k(CC)], w=["vel"])
    ts(T.a1[:, 72:80:4], T.c64[:, 0:2], T.tt[:, 127:128], A.add, c(CC), A.add, r=["c64", "tt", k(CC)], w=["ver"])
    ts(T.ve0[:], T.se[:, 15::16], IB16, A.mult, c(CC), A.add, r=["se", k(CC)], w=["ve0"])
    tt(T.a1[:, 0:64:4], T.ve0[:], T.uon[:], A.add, r=["ve0", "uon"], w=["ve"])

    mm(T.pm[:, 0:128], T.ident[:], T.adjl[:], True, False, ["ident", "adjk", "adjl"], "pm", 128)
    mm(T.pm[:, 0:64], T.sel1[:], T.land1[:, 4:68], False, False, ["sel1", "land1"], "pm", 256)
    mm(T.pm[:, 64:128], T.sel0[:], T.land1[:, 4:68], False, True, ["sel0", "land1"], "pm", 256)
    mm(T.pp[:, 256:320], T.inr1[:], T.land1[:, 4:68], False, False, ["inr1", "land1"], "pp", 256)
    VE = ["ve", "vel", "ver"]
    C127 = ["c127a", "c127b", "land1", "landx"]
    inr = T.land1[:, 68:69]
    if rank == N - 1:
        ts(T.a0[:, 1::4], T.c127[:], inr, A.mult, r=C127, w=["a0"])
    else:
        r3 = (T.land1[:, 0:1], T.landx[:, 0:1], T.land1[:, 69:70])[rank]
        ts(T.a0[:, 1::4], T.c127[:], inr, A.mult, r3, A.add, r=C127, w=["a0"])
    if rank not in (0, N - 1):
        l0 = T.land1[:, 0:1] if rank == 1 else T.landx[:, 0:1]
        ts(T.a1[:, 0::4], T.a1[:, 0::4], l0, A.subtract, r=["land1"], w=VE)
    scan(T.b1[:], T.a0[:], T.a1[:], A.add, A.max, r=["a0", "a1"] + VE, w=["b1"], n=80)
    first()
    scan(T.sin[:], T.mb16[:, 0:128], T.pm[:, 0:128], A.mult, A.add, r=["mb16"], w=["sin"], b="pm", n=128)
    I2 = T.sin[:, 79:128:16]
    ts(I0, T.b1[:, 65:80:4], B16, A.mult, r=["b1", "bb"], w=["i0"])
    act(I4, I2, IB16, r=["sin", "ib"], w=["i4"])
    tt(I1, I0, T.sin[:, 15:64:16], A.add, r=["i0", "sin"], w=["i1"])
    ts(I3, I1, B16, A.max, c(B127), A.min, r=["i1", k(B127)], w=["i3"])
    tt(T.xo[:], I3, I2, A.add, r=["i3", "sin"], w=["xo"])
    ts(T.uo16[:, 16:20], I3, IB16, A.mult, r=["i3"], w=["uoi"])
    ts(T.xo16[:, 16:20], T.xo[:], IB16, A.mult, r=["xo"], w=["xoi"])
    cp(T.loe[:, 128:160], I4.indirect(T.offe[:, 0:2]), r=["i4", "offe"], w=["loi"], n=gat(32))
    ts(T.zz[:, 16:20], I4, 300.0, A.is_equal, c(N8B), A.mult, r=["i4", k(N8B)], w=["zzi"])
    act(T.y1[:, 16:18], T.ii[:, 16:18], 1.0, -4096.0, r=["i4"], w=["y0b"])
    act(T.y1[:, 18:20], T.ii[:, 18:20], 1.0, 3584.0, r=["i4"], w=["y0c"])
    limits(16, 20, ["y0b", "y0c"], "i")
    tt(T.thg[:, 16:20], T.thl[:, 16:20], T.zz[:, 16:20], A.add, r=["thli", "zzi"], w=["thgi"])

    SC = scatterings(CUT2)

    U = T.sc[:, 7:160:8]
    act(T.pay[:], T.pp[:, 0:320], 1.0, c(PAYB), w=["pay"], b="pp", n=320)
    tt(T.fl[:, 40:60], U, T.thr[:], A.is_ge, r=SC + ["thr", "thri"], w=["f2"])
    tt(T.fl[:, 0:20], U, T.thl[:], A.is_lt, r=SC + ["thl", "thli"], w=["f0", "fr", "fl"])
    tt(T.fl[:, 20:40], U, T.thg[:], A.is_ge, r=SC + ["thg", "thgi", "al2", "fq"], w=["f1"])
    scan(T.fs[:], T.d0b[:], T.fl[:], A.min, A.add, r=["d0b", "f0", "f1", "f2"], w=["fs"])
    for j in (2, 0, 1):
        mm(T.pr[:, j + 1:80:4], T.r1[:], T.fl[:, 20 * j:20 * j + 20], False, False, ["r1", "f%d" % j], "pr")
    mm(T.pr[:, 2:80:4], T.nt2[:], T.fl[:, 40:60], False, False, ["nt2", "f2"], "pr")
    mm(T.pr[:, 2:80:4], T.nblk[:], T.fs[:, 40:60], False, False, ["nblk", "fs"], "pr")
    for j in range(3):
        mm(T.pr[:, j + 1:80:4], T.blk[:], T.fs[:, 20 * j:20 * j + 20], False, j == 2, ["blk", "fs"], "pr")
    mm(T.pm[:, 0:2], T.blk[:], T.fs[:, 39:60:20], True, False, ["blk", "fs"], "pm")
    mm(T.pm[:, 0:1], T.nblk[:], T.fs[:, 59:60], False, True, ["nblk", "fs"], "pm")
    scan(T.mx[:], T.d0d[:], T.pr[:, 0:80], A.min, A.max, r=["d0d"], w=["mx"], b="pr", n=80)
    act(T.win2[:, 640:641], T.pm[:, 1:2], 1.0, float(LB), r=["cnt"], w=["cn0"], b="pm")
    act(T.win2[:, 641:642], T.pm[:, 1:2], -1.0, float(RB - LB), r=["cnt"], w=["cn1"], b="pm")
    act(c(EC), T.pm[:, 0:1], -1.0, float(LB - SB), w=[k(EC)], b="pm")
    act(c(NS), T.pm[:, 0:1], w=[k(NS)], b="pm")
    cp(T.dst[:], T.mx[:, 3:80:4], r=["mx"], w=["dst"])
    cp(T.win2[:, 0:640].indirect(T.dst[:]), T.pay[:], r=["pay", "dst"], w=["win2", "win2b"], n=60 + 3.8 * 320)
    send([(T.win2[:, 608:644], [(right, T.win2[:, LB:LB + 36])], eng[:half]),
          (T.win2[:, 316:352], [(left, T.win2[:, RB - 4:RB + 32])], eng[half:])], "x3", ["win2", "cn0", "cn1"],
         ["sent3"])
    arrive("land2", "x3", ne, ["sent3"], FAR)
    ts(O0, T.jt[:], c(NS), A.is_ge, c(EC), A.mult, r=["jt", k(NS), k(EC)], w=["o0"])
    ts(O1, T.jt[:], float(SB), A.add, r=["jt"], w=["o1"])
    tt(O2, O0, O1, A.add, r=["o0", "o1"], w=["o2"])
    ts(O0, O2, T.win2[:, LB + 32:LB + 33], A.is_ge, T.win2[:, LB + 33:LB + 34], A.mult, r=["o2", "land2"], w=["o0"])
    act(T.win2[:, LB:LB + 32], T.win2[:, LB:LB + 32], 1.0, c(M8), r=["land2", k(M8)], w=["fixl"])
    act(T.win2[:, RB:RB + 32], T.win2[:, RB:RB + 32], 1.0, c(P8), r=["land2", k(P8)], w=["fixr"])
    tt(O3, O0, O2, A.add, r=["o0", "o2"], w=["o3"])
    ts(T.o16[:], O3, float(ZC), A.min, r=["o3"], w=["o16"])
    W2 = ["o16", "win2", "fixl", "fixr", "zc", "cn0", "cn1", "land2"]
    cp(T.res[:, 0:128], T.win2[:].indirect(T.o16[:, 0:8]), r=W2, w=["res"], n=gat(128))
    act(T.res[:, 128:256], T.win2[:].indirect(T.o16[:, 8:16]), r=W2, w=["res2"], n=gat(128))
    dma("y", T.yx[:], T.res[0::16, :], r=["res", "res2"])
    dma("s", T.yv[:], T.res[1::16, :], r=["res", "res2"])
    dma("y", T.yw[:], T.res[2::16, :], r=["res", "res2"])

    n_ops = len(ops)
    deps = [list(o["dep"].items()) for o in ops]
    users = [[] for _ in ops]
    for i, dd in enumerate(deps):
        for d, _ in dd:
            users[d].append(i)
    hold, late, where = [o["hold"] for o in ops], [o["lat"] for o in ops], [o["e"] for o in ops]

    def place(prio):
        todo = [len(dd) for dd in deps]
        ready = [i for i in range(n_ops) if not todo[i]]
        at, busy = [0.0] * n_ops, {e: [] for e in Q}
        while ready:
            i = max(ready, key=lambda x: prio[x])
            ready.remove(i)
            t = 0.0
            for d, wait in deps[i]:
                t = max(t, at[d] + late[d] + (LAT if wait else 0))
            if where[i] is not None:
                b, j = busy[where[i]], 0
                while j < len(b) and t + hold[i] > b[j][0]:
                    t = max(t, b[j][1])
                    j += 1
                b.insert(j, (t, t + hold[i]))
            at[i] = t
            for u in users[i]:
                todo[u] -= 1
                if not todo[u]:
                    ready.append(u)
        return sorted(range(n_ops), key=lambda x: (at[x], x))

    def length(order):
        total = 0.0
        for lat, pe in TRY:
            end, free = [0.0] * n_ops, {e: 0.0 for e in Q}
            for i in order:
                e = where[i]
                t = free[e] if e else 0.0
                for d, wait in deps[i]:
                    if wait:
                        t = max(t, end[d] + lat)
                f = pe if e == "p" else 1.0
                if e:
                    free[e] = t + hold[i] * f
                end[i] = t + late[i] * f
            total += max(end)
        return total

    level = [0.0] * n_ops
    for i in range(n_ops - 1, -1, -1):
        level[i] += late[i]
        for d, wait in deps[i]:
            level[d] = max(level[d], level[i] + (LAT if wait else 0))
    rng = np.random.default_rng(rank)
    order = place(level)
    best = length(order)
    for turn in range(ROUNDS):
        moved = list(level)
        for i in rng.integers(0, n_ops, 6):
            moved[int(i)] += float(rng.normal(0, 1)) * (300 if turn % 2 else 2500)
        if turn % 3 == 0:
            a, shift = int(rng.integers(0, n_ops)), float(rng.normal(0, 500))
            for i in range(a, min(n_ops, a + int(rng.integers(3, 30)))):
                moved[i] += shift
        cand = place(moved)
        size = length(cand)
        if size <= best:
            level, order, best = moved, cand, size
    count, clock, tok = {}, {e: {} for e in Q}, {}
    nd = 0
    for i in order:
        o = ops[i]
        e = o["e"]
        if e is None:
            s, n = o["fn"]
            if n:
                count[s] = n
                tok[i] = (s, n, {})
            continue
        for s, v, clk in sorted([tok[d] for d, wait in deps[i] if wait and d in tok], key=lambda x: -x[1]):
            if clock[e].get(s, 0) < v:
                Q[e].wait_ge(sem[s], v)
                for n, x in clk.items():
                    clock[e][n] = max(clock[e].get(n, 0), x)
                clock[e][s] = v
        if o["kind"] == "send":
            g.remote_dma_fused(o["fn"][0], local_sem=sem.ls)
            count["ls"] = count.get("ls", 0) + o["fn"][1]
            continue
        s, inc = (own[e], 1) if o["kind"] == "op" else ("d%d" % nd, 16)
        nd += o["kind"] == "dma"
        o["fn"]().then_inc(sem[s], inc)
        count[s] = count.get(s, 0) + inc
        tok[i] = (s, count[s], dict(clock[e]))
    for s, n in count.items():
        g.wait_ge(sem[s], n)
